import numpy as np
import ml_dtypes


def mxq(x, axis, fmt="e4m3"):
    dtype, down = {"e4m3": (ml_dtypes.float8_e4m3fn, 7), "e5m2": (ml_dtypes.float8_e5m2, 14)}[fmt]
    v = np.moveaxis(np.asarray(x, np.float32).astype(ml_dtypes.bfloat16).astype(np.float64), axis, -1)
    blocks = v.reshape(v.shape[:-1] + (-1, 32))
    amax = np.abs(blocks).max(-1, keepdims=True)
    byte = np.maximum(np.where(amax > 0, np.frexp(amax)[1] - 1 + 127, 0) - down, 1)
    scale = np.exp2(byte - 127.0)
    codes = (blocks / scale).astype(np.float32).astype(dtype).astype(np.float64)
    return np.moveaxis((codes * scale).reshape(v.shape), -1, axis)


WIDE = False


def mx_kscale(k):
    if not WIDE:
        return np.ones(k)
    levels = np.array([10, -10, 5, -5, 0])
    if k % 512:
        return np.exp2(np.random.permutation(np.resize(levels, k // 32))).repeat(32)
    a = np.empty((k // 512, 16))
    for p in range(k // 512):
        a[p, :8] = np.random.permutation(np.resize(levels, 8))
        for g in range(8):
            far = levels[np.abs(levels - a[p, g]) >= 10]
            a[p, g + 8] = far[np.random.randint(len(far))]
    return np.exp2(a.ravel()).repeat(32)


def f64(x):
    return np.asarray(x).astype(np.float64)


def striped(idx):
    return np.tile(idx.reshape(-1, 16).T, (8, 1)).astype(np.uint16)


def unstriped(offs):
    return offs[:16].T.reshape(-1).astype(np.int64)


def pack_weight(w):
    k, n = w.shape
    w = f64(np.asarray(w, np.float32).astype(ml_dtypes.bfloat16)).reshape(k // 32, 32, n)
    amax = np.abs(w).max(1)
    byte = np.clip(np.where(amax > 0, np.frexp(amax)[1] - 1 + 127 - 7, 1), 1, 254)
    scaled = (w * np.exp2(127.0 - byte)[:, None, :]).reshape(k, n).astype(np.float32)
    words = np.ascontiguousarray(scaled.reshape(k // 512, 128, 4, n).transpose(0, 1, 3, 2)).astype(ml_dtypes.float8_e4m3fn).view(np.uint8)
    return words, np.ascontiguousarray(byte.astype(np.uint8).reshape(k // 512, 16, n))


def unpack_weight(words, scales):
    g, p, n, _ = words.shape
    vals = np.ascontiguousarray(words).view(ml_dtypes.float8_e4m3fn).astype(np.float64) * np.repeat(np.exp2(scales.astype(np.float64) - 127.0), 8, axis=1)[..., None]
    return vals.transpose(0, 1, 3, 2).reshape(g * 512, n)


def relu(v):
    return np.maximum(v, 0.0)


K, T, S, H, V, W = 1024, 1024, 512, 512, 512, 2048


def setup_inputs():
    n = np.random.standard_normal
    s = mx_kscale(K)[:, None]
    u = mx_kscale(H)
    packed_xT = pack_weight(n((K, T)) * s)
    packed_eT = pack_weight(n((H, W)) / np.sqrt(H) / u[:, None])
    return {
        "x_words": packed_xT[0],
        "x_scales": packed_xT[1],
        "w1": (n((K, H)) / np.sqrt(K) / s * u).astype(np.float32),
        "e_words": packed_eT[0],
        "e_scales": packed_eT[1],
        "ago": (np.random.uniform(0.0, 3.0, (S, V))).astype(np.float32),
        "before": ((np.random.uniform(size=(S, V)) < 0.6) * 1.0).astype(np.float32),
        "mu": (np.random.uniform(20.0, 80.0, (S, 1))).astype(np.float32),
        "offs": striped(np.random.permutation(T)[:S]),
        "past": striped(np.random.permutation(W)[:V]),
    }


def reference(x_words, x_scales, w1, e_words, e_scales, ago, before, mu, offs, past):
    xq = unpack_weight(x_words, x_scales)[:, unstriped(offs)]
    h = relu(mxq(f64(w1), 0, "e4m3").T @ xq)
    e_past = unpack_weight(e_words, e_scales)[:, unstriped(past)]
    y = relu(mxq(h, 0, "e4m3").T @ e_past)
    gg = (y * (np.exp(-0.7 * f64(ago)))) * f64(before)
    lam = gg.sum(axis=1, keepdims=True) + f64(mu)
    return np.log(50.0 * (gg / lam) + 0.05)

@@ -1,0 +1,160 @@
+from contextlib import ExitStack
+
+import concourse.mybir as mybir
+
+K, T, S, H, V, W = 1024, 1024, 512, 512, 512, 2048
+FLOPS = 2 * K * H * S + 2 * H * S * V
+
+F32 = mybir.dt.float32
+BF16 = mybir.dt.bfloat16
+I32 = mybir.dt.int32
+U32 = mybir.dt.uint32
+U16 = mybir.dt.uint16
+U8 = mybir.dt.uint8
+FP8X4 = mybir.dt.float8_e4m3fn_x4
+ALU = mybir.AluOpType
+ACT = mybir.ActivationFunctionType
+
+P = 128
+PACK = 4
+K_PASS = P * PACK
+PASSES = K // K_PASS
+BLOCKS = S // P
+LIST_ROWS = 16
+SCALAR_M = [80, 48]
+
+
+def tile_picked_yhawem_log_p_kernel(
+    tc, x_words, x_scales, w1, e_words, e_scales, ago, before, mu, offs, past, out
+):
+    nc = tc.nc
+    with ExitStack() as ctx:
+        keep = ctx.enter_context(tc.tile_pool(name="keep", bufs=1))
+        psum = ctx.enter_context(tc.psum_pool(name="psum", bufs=1))
+
+        def tile(shape, dtype, name):
+            return keep.tile(shape, dtype, name=name, align_bytes=64)
+
+        x_scale_table = tile([P, T], U8, "x_scale_table")
+        e_scale_table = tile([P, W], U8, "e_scale_table")
+        nc.vector.memset(x_scale_table[:].bitcast(I32), 0)
+        nc.gpsimd.memset(e_scale_table[:].bitcast(I32), 0)
+
+        x_list = tile([P, S // LIST_ROWS], U16, "x_list")
+        nc.sync.dma_start(x_list[:], offs)
+        for q in range(4):
+            nc.scalar.dma_start(
+                x_scale_table[32 * q : 32 * q + 4 * PASSES, :].bitcast(I32),
+                x_scales[:, 4 * q : 4 * q + 4, :].bitcast(I32),
+            )
+        w_raw = []
+        for g in range(PASSES):
+            raw = tile([P, PACK, H], F32, f"w_raw{g}")
+            nc.sync.dma_start(raw[:], w1[g * K_PASS : (g + 1) * K_PASS, :].rearrange("(p j) c -> p j c", j=PACK))
+            w_raw.append(raw)
+        e_list = tile([P, V // LIST_ROWS], U16, "e_list")
+        nc.sync.dma_start(e_list[:], past)
+        for q in range(4):
+            nc.gpsimd.dma_start(
+                e_scale_table[32 * q : 32 * q + 4, :].bitcast(I32),
+                e_scales[0, 4 * q : 4 * q + 4, :].bitcast(I32),
+            )
+        mu_sb = tile([P, BLOCKS], F32, "mu_sb")
+        with nc.allow_non_contiguous_dma(reason="one background rate a row"):
+            nc.gpsimd.dma_start(mu_sb[:], mu.rearrange("(b p) o -> p (b o)", p=P))
+        x_table = []
+        for g in range(PASSES):
+            table = tile([P, T], U32, f"x_table{g}")
+            nc.sync.dma_start(table[:].bitcast(I32), x_words[g].rearrange("p n t -> p (n t)").bitcast(I32))
+            x_table.append(table)
+        e_table = tile([P, W], U32, "e_table")
+        nc.sync.dma_start(e_table[:].bitcast(I32), e_words[0].rearrange("p n t -> p (n t)").bitcast(I32))
+        ago_sb = []
+        for u in range(BLOCKS // 2):
+            pair = tile([P, 2, V], F32, f"ago{u}")
+            nc.sync.dma_start(pair[:], ago[2 * u * P : 2 * (u + 1) * P, :].rearrange("(b p) v -> p b v", p=P))
+            ago_sb.append(pair)
+        before_sb = []
+        for b in range(BLOCKS):
+            rows = tile([P, V], F32, f"before{b}")
+            nc.sync.dma_start(rows[:], before[b * P : (b + 1) * P, :])
+            before_sb.append(rows)
+
+        x_scale = tile([P, S], U8, "x_scale")
+        nc.vector.tensor_copy(x_scale[:], x_scale_table[:].indirect(x_list[:]))
+        e_scale = tile([P, V], U8, "e_scale")
+        nc.vector.tensor_copy(e_scale[:], e_scale_table[:].indirect(e_list[:]))
+
+        w_codes, w_scale = [], []
+        for g in range(PASSES):
+            grouped = tile([P, PACK, P, PACK], BF16, f"w_grouped{g}")
+            dst = grouped[:].rearrange("p t m j -> p m t j")
+            src = w_raw[g][:].rearrange("p j (m t) -> p m t j", t=PACK)
+            cut = SCALAR_M[g]
+            nc.scalar.copy(dst[:, :cut], src[:, :cut])
+            nc.vector.tensor_copy(dst[:, cut:], src[:, cut:])
+            codes = tile([P, H], U32, f"w_codes{g}")
+            scale = tile([P, H], U8, f"w_scale{g}")
+            nc.vector.quantize_mx(codes[:].bitcast(FP8X4), scale[:], grouped[:].rearrange("p t m j -> p (t m j)"))
+            w_codes.append(codes)
+            w_scale.append(scale)
+
+        x_codes = {}
+        for b in range(BLOCKS):
+            entries = x_list[:, b * P // LIST_ROWS : (b + 1) * P // LIST_ROWS]
+            for g in range(PASSES):
+                x_codes[b, g] = tile([P, P], U32, f"x_codes{b}_{g}")
+                nc.vector.tensor_copy(x_codes[b, g][:], x_table[g][:].indirect(entries))
+        e_codes = tile([P, V], U32, "e_codes")
+        nc.vector.tensor_copy(e_codes[:], e_table[:].indirect(e_list[:]))
+
+        scores = []
+        for b in range(BLOCKS):
+            h_acc = psum.tile([P, PACK, P], F32, name=f"h_acc{b}")
+            for t in range(PACK):
+                for g in range(PASSES):
+                    nc.tensor.matmul_mx(
+                        out=h_acc[:, t, :],
+                        lhsT=w_codes[g][:, t * P : (t + 1) * P].bitcast(FP8X4),
+                        lhsT_scale=w_scale[g][:, t * P : (t + 1) * P],
+                        rhs=x_codes[b, g][:].bitcast(FP8X4),
+                        rhs_scale=x_scale[4 * g : P, b * P : (b + 1) * P],
+                        start=(g == 0),
+                        stop=(g == PASSES - 1),
+                    )
+            h_grouped = tile([P, P, PACK], BF16, f"h_grouped{b}")
+            nc.scalar.activation(h_grouped[:], h_acc[:].rearrange("p t n -> p n t"), ACT.Relu)
+            h_codes = tile([P, P], U32, f"h_codes{b}")
+            h_scale = tile([P, P], U8, f"h_scale{b}")
+            nc.vector.quantize_mx(h_codes[:].bitcast(FP8X4), h_scale[:], h_grouped[:].rearrange("p n t -> p (n t)"))
+            y_acc = psum.tile([P, V], F32, name=f"y_acc{b}")
+            nc.tensor.matmul_mx(
+                out=y_acc[:],
+                lhsT=h_codes[:].bitcast(FP8X4),
+                lhsT_scale=h_scale[:],
+                rhs=e_codes[:].bitcast(FP8X4),
+                rhs_scale=e_scale[:],
+                start=True,
+                stop=True,
+            )
+            scores.append(y_acc)
+
+        decay = []
+        for u in range(BLOCKS // 2):
+            pair = tile([P, 2, V], F32, f"decay{u}")
+            nc.scalar.activation(pair[:], ago_sb[u][:], ACT.Exp, scale=-0.7)
+            decay.append(pair)
+
+        for b in range(BLOCKS):
+            decayed = tile([P, V], F32, f"decayed{b}")
+            nc.vector.scalar_tensor_tensor(decayed[:], scores[b][:], 0.0, decay[b // 2][:, b % 2, :], ALU.max, ALU.mult)
+            gg = tile([P, V], F32, f"gg{b}")
+            total = tile([P, 1], F32, f"total{b}")
+            nc.vector.scalar_tensor_tensor(gg[:], decayed[:], 1.0, before_sb[b][:], ALU.mult, ALU.mult, accum_out=total[:])
+            lam = tile([P, 1], F32, f"lam{b}")
+            nc.vector.tensor_scalar(lam[:], total[:], mu_sb[:, b : b + 1], 1.0 / 50.0, ALU.add, ALU.mult)
+            factor = tile([P, 1], F32, f"factor{b}")
+            nc.vector.reciprocal(factor[:], lam[:])
+            result = tile([P, V], F32, f"result{b}")
+            nc.scalar.activation(result[:], gg[:], ACT.Ln, bias=0.05, scale=factor[:])
+            nc.sync.dma_start(out[b * P : (b + 1) * P, :], result[:])

@@ -1,6 +1,7 @@
 from contextlib import ExitStack
 
 import concourse.mybir as mybir
+from concourse.masks import make_identity
 
 K, T, S, H, V, W = 1024, 1024, 512, 512, 512, 2048
 FLOPS = 2 * K * H * S + 2 * H * S * V
@@ -21,7 +22,9 @@ K_PASS = P * PACK
 PASSES = K // K_PASS
 BLOCKS = S // P
 LIST_ROWS = 16
-SCALAR_M = [80, 48]
+SCALAR_M = [128,64,20]
+RELU_ON_VECTOR = []
+STORE_PARTS = [1,1,1,2]
 
 
 def tile_picked_yhawem_log_p_kernel(
@@ -32,129 +35,232 @@ def tile_picked_yhawem_log_p_kernel(
         keep = ctx.enter_context(tc.tile_pool(name="keep", bufs=1))
         psum = ctx.enter_context(tc.psum_pool(name="psum", bufs=1))
 
-        def tile(shape, dtype, name):
-            return keep.tile(shape, dtype, name=name, align_bytes=64)
-
-        x_scale_table = tile([P, T], U8, "x_scale_table")
-        e_scale_table = tile([P, W], U8, "e_scale_table")
-        nc.vector.memset(x_scale_table[:].bitcast(I32), 0)
-        nc.gpsimd.memset(e_scale_table[:].bitcast(I32), 0)
+        def tile(shape, dtype, name, tag=None):
+            return keep.tile(shape, dtype, name=name, tag=tag or name, align_bytes=64)
 
         x_list = tile([P, S // LIST_ROWS], U16, "x_list")
-        nc.sync.dma_start(x_list[:], offs)
-        for q in range(4):
-            nc.scalar.dma_start(
-                x_scale_table[32 * q : 32 * q + 4 * PASSES, :].bitcast(I32),
-                x_scales[:, 4 * q : 4 * q + 4, :].bitcast(I32),
-            )
-        w_raw = []
-        for g in range(PASSES):
-            raw = tile([P, PACK, H], F32, f"w_raw{g}")
-            nc.sync.dma_start(raw[:], w1[g * K_PASS : (g + 1) * K_PASS, :].rearrange("(p j) c -> p j c", j=PACK))
-            w_raw.append(raw)
         e_list = tile([P, V // LIST_ROWS], U16, "e_list")
-        nc.sync.dma_start(e_list[:], past)
-        for q in range(4):
-            nc.gpsimd.dma_start(
-                e_scale_table[32 * q : 32 * q + 4, :].bitcast(I32),
-                e_scales[0, 4 * q : 4 * q + 4, :].bitcast(I32),
-            )
-        mu_sb = tile([P, BLOCKS], F32, "mu_sb")
-        with nc.allow_non_contiguous_dma(reason="one background rate a row"):
-            nc.gpsimd.dma_start(mu_sb[:], mu.rearrange("(b p) o -> p (b o)", p=P))
-        x_table = []
-        for g in range(PASSES):
-            table = tile([P, T], U32, f"x_table{g}")
-            nc.sync.dma_start(table[:].bitcast(I32), x_words[g].rearrange("p n t -> p (n t)").bitcast(I32))
-            x_table.append(table)
+        x_scale_table = tile([P, T], U8, "x_scale_table")
+        e_scale_table = tile([P, W], U8, "e_scale_table")
+        x_table = [tile([P, T], U32, f"x_table{g}") for g in range(PASSES)]
         e_table = tile([P, W], U32, "e_table")
-        nc.sync.dma_start(e_table[:].bitcast(I32), e_words[0].rearrange("p n t -> p (n t)").bitcast(I32))
-        ago_sb = []
-        for u in range(BLOCKS // 2):
-            pair = tile([P, 2, V], F32, f"ago{u}")
-            nc.sync.dma_start(pair[:], ago[2 * u * P : 2 * (u + 1) * P, :].rearrange("(b p) v -> p b v", p=P))
-            ago_sb.append(pair)
-        before_sb = []
-        for b in range(BLOCKS):
-            rows = tile([P, V], F32, f"before{b}")
-            nc.sync.dma_start(rows[:], before[b * P : (b + 1) * P, :])
-            before_sb.append(rows)
-
+        w_raw = [tile([P, PACK, H], F32, "w_raw0")]
+        w_half = [tile([P, PACK, H // 2], F32, f"w_half{u}") for u in range(2)]
+        mu_sb = tile([P, BLOCKS], F32, "mu_sb")
+        ago_sb = [tile([P, V], F32, f"ago{b}") for b in range(BLOCKS)]
+        before_sb = [tile([P, V], F32, f"before{b}") for b in range(BLOCKS)]
         x_scale = tile([P, S], U8, "x_scale")
-        nc.vector.tensor_copy(x_scale[:], x_scale_table[:].indirect(x_list[:]))
         e_scale = tile([P, V], U8, "e_scale")
-        nc.vector.tensor_copy(e_scale[:], e_scale_table[:].indirect(e_list[:]))
-
-        w_codes, w_scale = [], []
-        for g in range(PASSES):
-            grouped = tile([P, PACK, P, PACK], BF16, f"w_grouped{g}")
-            dst = grouped[:].rearrange("p t m j -> p m t j")
-            src = w_raw[g][:].rearrange("p j (m t) -> p m t j", t=PACK)
-            cut = SCALAR_M[g]
-            nc.scalar.copy(dst[:, :cut], src[:, :cut])
-            nc.vector.tensor_copy(dst[:, cut:], src[:, cut:])
-            codes = tile([P, H], U32, f"w_codes{g}")
-            scale = tile([P, H], U8, f"w_scale{g}")
-            nc.vector.quantize_mx(codes[:].bitcast(FP8X4), scale[:], grouped[:].rearrange("p t m j -> p (t m j)"))
-            w_codes.append(codes)
-            w_scale.append(scale)
-
-        x_codes = {}
-        for b in range(BLOCKS):
-            entries = x_list[:, b * P // LIST_ROWS : (b + 1) * P // LIST_ROWS]
-            for g in range(PASSES):
-                x_codes[b, g] = tile([P, P], U32, f"x_codes{b}_{g}")
-                nc.vector.tensor_copy(x_codes[b, g][:], x_table[g][:].indirect(entries))
+        x_first = tile([P, S], U32, "x_first")
+        x_second = [tile([P, P], U32, f"x_second{b}") for b in range(BLOCKS)]
         e_codes = tile([P, V], U32, "e_codes")
-        nc.vector.tensor_copy(e_codes[:], e_table[:].indirect(e_list[:]))
+        w_grouped = [tile([P, PACK, P, PACK], BF16, f"w_grouped{g}") for g in range(PASSES)]
+        w_codes = [tile([P, H], U32, f"w_codes{g}") for g in range(PASSES)]
+        w_scale = [tile([P, H], U8, f"w_scale{g}") for g in range(PASSES)]
+        h_all = tile([P, BLOCKS, P], U32, "h_all", tag="e_table")
+        h_codes = [h_all[:, b, :] for b in range(BLOCKS)]
+        h_grouped = [tile([P, P, PACK], BF16, f"h_grouped{b}") for b in range(BLOCKS)]
+        h_scale = [tile([P, P], U8, f"h_scale{b}") for b in range(BLOCKS)]
+        decay = [tile([P, V], F32, f"decay{b}") for b in range(BLOCKS)]
+        partial = [tile([P, V], F32, f"partial{b}") for b in range(BLOCKS)]
+        mu_rows = tile([P, P], F32, "mu_rows")
+        identity = tile([P, P], F32, "identity")
 
-        scores = []
-        for b in range(BLOCKS):
+        def load_x(g):
+            nc.sync.dma_start(x_table[g][:].bitcast(I32), x_words[g].rearrange("p n t -> p (n t)").bitcast(I32))
+
+        def load_w(g):
+            nc.sync.dma_start(w_raw[g][:], w1[g * K_PASS : (g + 1) * K_PASS, :].rearrange("(p j) c -> p j c", j=PACK))
+
+        def load_ago(u):
+            nc.sync.dma_start(ago_sb[u][:], ago[u * P : (u + 1) * P, :])
+
+        def load_before(b):
+            nc.sync.dma_start(before_sb[b][:], before[b * P : (b + 1) * P, :])
+
+        def load_w_half(u):
+            cols = slice(u * H // 2, (u + 1) * H // 2)
+            nc.sync.dma_start(w_half[u][:], w1[K_PASS:, cols].rearrange("(p j) c -> p j c", j=PACK))
+
+        def cast_piece(raw, dst, cut):
+            src = raw[:].rearrange("p j (m t) -> p m j t", t=PACK)
+            if cut > 0:
+                nc.scalar.copy(dst[:, :cut], src[:, :cut])
+            if cut < src.shape[1]:
+                nc.vector.tensor_copy(dst[:, cut:], src[:, cut:])
+
+        def cast_w(g):
+            dst = w_grouped[g][:].rearrange("p t m j -> p m j t")
+            if g == 0:
+                cast_piece(w_raw[0], dst, SCALAR_M[0])
+            else:
+                cast_piece(w_half[0], dst[:, : P // 2], SCALAR_M[1])
+                cast_piece(w_half[1], dst[:, P // 2 :], SCALAR_M[2])
+
+        def quantize_w(g):
+            nc.vector.quantize_mx(
+                w_codes[g][:].bitcast(FP8X4), w_scale[g][:], w_grouped[g][:].rearrange("p t m j -> p (t m j)")
+            )
+
+        def gather_x(b):
+            entries = x_list[:, b * P // LIST_ROWS : (b + 1) * P // LIST_ROWS]
+            nc.vector.tensor_copy(x_second[b][:], x_table[1][:].indirect(entries))
+
+        def gather_first(b):
+            entries = x_list[:, b * P // LIST_ROWS : (b + 1) * P // LIST_ROWS]
+            nc.vector.tensor_copy(x_first[b][:], x_table[0][:].indirect(entries))
+
+        def warm(n):
+            for r in range(n):
+                nc.tensor.matmul_mx(
+                    out=spare[:],
+                    lhsT=w_codes[0][:, :P].bitcast(FP8X4),
+                    lhsT_scale=w_scale[0][:, :P],
+                    rhs=w_codes[0][:].bitcast(FP8X4),
+                    rhs_scale=w_scale[0][:],
+                    start=True,
+                    stop=True,
+                )
+
+        def hidden(b):
             h_acc = psum.tile([P, PACK, P], F32, name=f"h_acc{b}")
+            moving = [x_first[:, b * P : (b + 1) * P], x_second[b][:]]
             for t in range(PACK):
                 for g in range(PASSES):
                     nc.tensor.matmul_mx(
                         out=h_acc[:, t, :],
                         lhsT=w_codes[g][:, t * P : (t + 1) * P].bitcast(FP8X4),
                         lhsT_scale=w_scale[g][:, t * P : (t + 1) * P],
-                        rhs=x_codes[b, g][:].bitcast(FP8X4),
+                        rhs=moving[g].bitcast(FP8X4),
                         rhs_scale=x_scale[4 * g : P, b * P : (b + 1) * P],
                         start=(g == 0),
                         stop=(g == PASSES - 1),
                     )
-            h_grouped = tile([P, P, PACK], BF16, f"h_grouped{b}")
-            nc.scalar.activation(h_grouped[:], h_acc[:].rearrange("p t n -> p n t"), ACT.Relu)
-            h_codes = tile([P, P], U32, f"h_codes{b}")
-            h_scale = tile([P, P], U8, f"h_scale{b}")
-            nc.vector.quantize_mx(h_codes[:].bitcast(FP8X4), h_scale[:], h_grouped[:].rearrange("p n t -> p (n t)"))
-            y_acc = psum.tile([P, V], F32, name=f"y_acc{b}")
+            if b in RELU_ON_VECTOR:
+                nc.vector.tensor_scalar_max(h_grouped[b][:], h_acc[:].rearrange("p t n -> p n t"), 0.0)
+            else:
+                nc.scalar.activation(h_grouped[b][:], h_acc[:].rearrange("p t n -> p n t"), ACT.Relu)
+
+        def quantize_h(b):
+            nc.vector.quantize_mx(
+                h_codes[b].bitcast(FP8X4), h_scale[b][:], h_grouped[b][:].rearrange("p n t -> p (n t)")
+            )
+
+        def score(b):
             nc.tensor.matmul_mx(
-                out=y_acc[:],
-                lhsT=h_codes[:].bitcast(FP8X4),
-                lhsT_scale=h_scale[:],
+                out=y_acc[b][:],
+                lhsT=h_codes[b].bitcast(FP8X4),
+                lhsT_scale=h_scale[b][:],
                 rhs=e_codes[:].bitcast(FP8X4),
                 rhs_scale=e_scale[:],
                 start=True,
                 stop=True,
             )
-            scores.append(y_acc)
 
-        decay = []
-        for u in range(BLOCKS // 2):
-            pair = tile([P, 2, V], F32, f"decay{u}")
-            nc.scalar.activation(pair[:], ago_sb[u][:], ACT.Exp, scale=-0.7)
-            decay.append(pair)
+        def decay_of(u):
+            nc.scalar.activation(decay[u][:], ago_sb[u][:], ACT.Exp, scale=-0.7)
 
-        for b in range(BLOCKS):
-            decayed = tile([P, V], F32, f"decayed{b}")
-            nc.vector.scalar_tensor_tensor(decayed[:], scores[b][:], 0.0, decay[b // 2][:, b % 2, :], ALU.max, ALU.mult)
-            gg = tile([P, V], F32, f"gg{b}")
-            total = tile([P, 1], F32, f"total{b}")
-            nc.vector.scalar_tensor_tensor(gg[:], decayed[:], 1.0, before_sb[b][:], ALU.mult, ALU.mult, accum_out=total[:])
+        def decayed_score(b):
+            nc.vector.scalar_tensor_tensor(partial[b][:], y_acc[b][:], 0.0, decay[b][:], ALU.max, ALU.mult)
+
+        def mask(b):
+            nc.gpsimd.tensor_tensor(partial[b][:], decay[b][:], before_sb[b][:], ALU.mult)
+
+        def finish(b, gg, total):
             lam = tile([P, 1], F32, f"lam{b}")
             nc.vector.tensor_scalar(lam[:], total[:], mu_sb[:, b : b + 1], 1.0 / 50.0, ALU.add, ALU.mult)
             factor = tile([P, 1], F32, f"factor{b}")
             nc.vector.reciprocal(factor[:], lam[:])
-            result = tile([P, V], F32, f"result{b}")
-            nc.scalar.activation(result[:], gg[:], ACT.Ln, bias=0.05, scale=factor[:])
-            nc.sync.dma_start(out[b * P : (b + 1) * P, :], result[:])
+            width = V // STORE_PARTS[b]
+            for c in range(STORE_PARTS[b]):
+                cols = slice(c * width, (c + 1) * width)
+                result = tile([P, width], F32, f"result{b}_{c}")
+                nc.scalar.activation(result[:], gg[:, cols], ACT.Ln, bias=0.05, scale=factor[:])
+                nc.sync.dma_start(out[b * P : (b + 1) * P, cols], result[:])
+
+        def share(b):
+            gg = tile([P, V], F32, f"gg{b}")
+            total = tile([P, 1], F32, f"total{b}")
+            nc.vector.scalar_tensor_tensor(gg[:], partial[b][:], 1.0, before_sb[b][:], ALU.mult, ALU.mult, accum_out=total[:])
+            finish(b, gg, total)
+
+        def share_masked(b):
+            gg = tile([P, V], F32, f"gg{b}")
+            total = tile([P, 1], F32, f"total{b}")
+            nc.vector.scalar_tensor_tensor(gg[:], y_acc[b][:], 0.0, partial[b][:], ALU.max, ALU.mult, accum_out=total[:])
+            finish(b, gg, total)
+
+        nc.vector.memset(x_scale_table[:].bitcast(I32), 0)
+        nc.gpsimd.memset(e_scale_table[:].bitcast(I32), 0)
+        nc.vector.memset(mu_rows[:], 0.0)
+        nc.sync.dma_start(x_list[:], offs)
+        nc.sync.dma_start(e_list[:], past)
+        for q in range(4):
+            nc.scalar.dma_start(
+                x_scale_table[32 * q : 32 * q + 4 * PASSES, :].bitcast(I32),
+                x_scales[:, 4 * q : 4 * q + 4, :].bitcast(I32),
+            )
+        load_w(0)
+        load_x(0)
+        load_w_half(0)
+        nc.sync.dma_start(mu_rows[:BLOCKS, :], mu.rearrange("(b p) o -> b (p o)", p=P))
+        make_identity(nc, identity[:])
+        mu_turned = psum.tile([P, P], F32, name="mu_turned", tag="y_acc3")
+        nc.tensor.transpose(mu_turned[:], mu_rows[:], identity[:])
+        nc.vector.tensor_copy(mu_sb[:], mu_turned[:, :BLOCKS])
+        spare = psum.tile([P, V], F32, name="spare", tag="y_acc0")
+        y_acc = [psum.tile([P, V], F32, name=f"y_acc{b}", tag=f"y_acc{b}") for b in range(BLOCKS)]
+        load_w_half(1)
+        load_x(1)
+        for q in range(4):
+            nc.sync.dma_start(
+                e_scale_table[32 * q : 32 * q + 4, :].bitcast(I32),
+                e_scales[0, 4 * q : 4 * q + 4, :].bitcast(I32),
+            )
+        load_ago(0)
+        nc.sync.dma_start(e_table[:].bitcast(I32), e_words[0].rearrange("p n t -> p (n t)").bitcast(I32))
+        load_ago(1)
+        load_ago(2)
+        load_ago(3)
+        load_before(0)
+        load_before(1)
+        load_before(2)
+        load_before(3)
+
+        nc.vector.tensor_copy(x_scale[:], x_scale_table[:].indirect(x_list[:]))
+        cast_w(0)
+        nc.vector.tensor_copy(x_first[:], x_table[0][:].indirect(x_list[:]))
+        quantize_w(0)
+        warm(3)
+        cast_w(1)
+        quantize_w(1)
+        gather_x(0)
+        hidden(0)
+        gather_x(1)
+        hidden(1)
+        gather_x(2)
+        hidden(2)
+        gather_x(3)
+        hidden(3)
+        nc.vector.tensor_copy(e_scale[:], e_scale_table[:].indirect(e_list[:]))
+        nc.vector.tensor_copy(e_codes[:], e_table[:].indirect(e_list[:]))
+        quantize_h(0)
+        score(0)
+        quantize_h(1)
+        score(1)
+        quantize_h(2)
+        score(2)
+        quantize_h(3)
+        score(3)
+        decay_of(0)
+        decay_of(1)
+        decay_of(2)
+        decay_of(3)
+        decayed_score(0)
+        share(0)
+        decayed_score(1)
+        share(1)
+        decayed_score(2)
+        share(2)
+        decayed_score(3)
+        share(3)

@@ -22,9 +22,8 @@ K_PASS = P * PACK
 PASSES = K // K_PASS
 BLOCKS = S // P
 LIST_ROWS = 16
-SCALAR_M = [128,64,20]
-RELU_ON_VECTOR = []
 STORE_PARTS = [1,1,1,2]
+EARLY_H = 0
 
 
 def tile_picked_yhawem_log_p_kernel(
@@ -44,8 +43,7 @@ def tile_picked_yhawem_log_p_kernel(
         e_scale_table = tile([P, W], U8, "e_scale_table")
         x_table = [tile([P, T], U32, f"x_table{g}") for g in range(PASSES)]
         e_table = tile([P, W], U32, "e_table")
-        w_raw = [tile([P, PACK, H], F32, "w_raw0")]
-        w_half = [tile([P, PACK, H // 2], F32, f"w_half{u}") for u in range(2)]
+        w_raw = [tile([P, PACK, H], F32, f"w_raw{g}") for g in range(PASSES)]
         mu_sb = tile([P, BLOCKS], F32, "mu_sb")
         ago_sb = [tile([P, V], F32, f"ago{b}") for b in range(BLOCKS)]
         before_sb = [tile([P, V], F32, f"before{b}") for b in range(BLOCKS)]
@@ -54,23 +52,28 @@ def tile_picked_yhawem_log_p_kernel(
         x_first = tile([P, S], U32, "x_first")
         x_second = [tile([P, P], U32, f"x_second{b}") for b in range(BLOCKS)]
         e_codes = tile([P, V], U32, "e_codes")
-        w_grouped = [tile([P, PACK, P, PACK], BF16, f"w_grouped{g}") for g in range(PASSES)]
-        w_codes = [tile([P, H], U32, f"w_codes{g}") for g in range(PASSES)]
-        w_scale = [tile([P, H], U8, f"w_scale{g}") for g in range(PASSES)]
-        h_all = tile([P, BLOCKS, P], U32, "h_all", tag="e_table")
-        h_codes = [h_all[:, b, :] for b in range(BLOCKS)]
+        w_grouped = [[tile([P, 2, P, PACK], BF16, f"w_grouped{g}_{u}") for u in range(2)] for g in range(PASSES)]
+        w_codes = [[tile([P, 2 * P], U32, f"w_codes{g}_{u}") for u in range(2)] for g in range(PASSES)]
+        w_scale = [[tile([P, 2 * P], U8, f"w_scale{g}_{u}") for u in range(2)] for g in range(PASSES)]
+        h_late = tile([P, BLOCKS, P], U32, "h_late", tag="e_table")
+        h_early = tile([P, BLOCKS, P], U32, "h_early")
+        h_codes = [(h_early if b < EARLY_H else h_late)[:, b, :] for b in range(BLOCKS)]
         h_grouped = [tile([P, P, PACK], BF16, f"h_grouped{b}") for b in range(BLOCKS)]
         h_scale = [tile([P, P], U8, f"h_scale{b}") for b in range(BLOCKS)]
         decay = [tile([P, V], F32, f"decay{b}") for b in range(BLOCKS)]
         partial = [tile([P, V], F32, f"partial{b}") for b in range(BLOCKS)]
         mu_rows = tile([P, P], F32, "mu_rows")
         identity = tile([P, P], F32, "identity")
+        ones = tile([P, 1], F32, "ones")
+        floor = tile([P, 1], F32, "floor")
+        clock = tile([P, 8], U32, "clock")
 
         def load_x(g):
             nc.sync.dma_start(x_table[g][:].bitcast(I32), x_words[g].rearrange("p n t -> p (n t)").bitcast(I32))
 
         def load_w(g):
-            nc.sync.dma_start(w_raw[g][:], w1[g * K_PASS : (g + 1) * K_PASS, :].rearrange("(p j) c -> p j c", j=PACK))
+            rows = slice(g * K_PASS, (g + 1) * K_PASS)
+            nc.sync.dma_start(w_raw[g][:], w1[rows, :].rearrange("(p j) c -> p j c", j=PACK))
 
         def load_ago(u):
             nc.sync.dma_start(ago_sb[u][:], ago[u * P : (u + 1) * P, :])
@@ -78,68 +81,72 @@ def tile_picked_yhawem_log_p_kernel(
         def load_before(b):
             nc.sync.dma_start(before_sb[b][:], before[b * P : (b + 1) * P, :])
 
-        def load_w_half(u):
-            cols = slice(u * H // 2, (u + 1) * H // 2)
-            nc.sync.dma_start(w_half[u][:], w1[K_PASS:, cols].rearrange("(p j) c -> p j c", j=PACK))
+        def load_x_scales(queue):
+            for q in range(4):
+                queue.dma_start(
+                    x_scale_table[32 * q : 32 * q + 4 * PASSES, :].bitcast(I32),
+                    x_scales[:, 4 * q : 4 * q + 4, :].bitcast(I32),
+                )
 
-        def cast_piece(raw, dst, cut):
-            src = raw[:].rearrange("p j (m t) -> p m j t", t=PACK)
-            if cut > 0:
-                nc.scalar.copy(dst[:, :cut], src[:, :cut])
-            if cut < src.shape[1]:
-                nc.vector.tensor_copy(dst[:, cut:], src[:, cut:])
+        def load_e_scales(queue):
+            for q in range(4):
+                queue.dma_start(
+                    e_scale_table[32 * q : 32 * q + 4, :].bitcast(I32),
+                    e_scales[0, 4 * q : 4 * q + 4, :].bitcast(I32),
+                )
 
-        def cast_w(g):
-            dst = w_grouped[g][:].rearrange("p t m j -> p m j t")
-            if g == 0:
-                cast_piece(w_raw[0], dst, SCALAR_M[0])
+        def load_e():
+            nc.sync.dma_start(e_table[:].bitcast(I32), e_words[0].rearrange("p n t -> p (n t)").bitcast(I32))
+
+        def load_mu():
+            nc.sync.dma_start(mu_rows[:BLOCKS, :], mu.rearrange("(b p) o -> b (p o)", p=P))
+
+        def cast_w(g, u, on_scalar):
+            dst = w_grouped[g][u][:].rearrange("p t m j -> p m j t")
+            src = w_raw[g][:].rearrange("p j (m t) -> p m j t", t=PACK)[:, :, :, 2 * u : 2 * u + 2]
+            if on_scalar:
+                nc.scalar.copy(dst, src)
             else:
-                cast_piece(w_half[0], dst[:, : P // 2], SCALAR_M[1])
-                cast_piece(w_half[1], dst[:, P // 2 :], SCALAR_M[2])
+                nc.vector.tensor_copy(dst, src)
 
-        def quantize_w(g):
+        def quantize_w(g, u):
             nc.vector.quantize_mx(
-                w_codes[g][:].bitcast(FP8X4), w_scale[g][:], w_grouped[g][:].rearrange("p t m j -> p (t m j)")
+                w_codes[g][u][:].bitcast(FP8X4), w_scale[g][u][:], w_grouped[g][u][:].rearrange("p t m j -> p (t m j)")
             )
 
         def gather_x(b):
             entries = x_list[:, b * P // LIST_ROWS : (b + 1) * P // LIST_ROWS]
             nc.vector.tensor_copy(x_second[b][:], x_table[1][:].indirect(entries))
 
-        def gather_first(b):
-            entries = x_list[:, b * P // LIST_ROWS : (b + 1) * P // LIST_ROWS]
-            nc.vector.tensor_copy(x_first[b][:], x_table[0][:].indirect(entries))
+        h_acc = [psum.tile([P, PACK, P], F32, name=f"h_acc{b}") for b in range(BLOCKS)]
 
-        def warm(n):
-            for r in range(n):
-                nc.tensor.matmul_mx(
-                    out=spare[:],
-                    lhsT=w_codes[0][:, :P].bitcast(FP8X4),
-                    lhsT_scale=w_scale[0][:, :P],
-                    rhs=w_codes[0][:].bitcast(FP8X4),
-                    rhs_scale=w_scale[0][:],
-                    start=True,
-                    stop=True,
-                )
-
-        def hidden(b):
-            h_acc = psum.tile([P, PACK, P], F32, name=f"h_acc{b}")
+        def hidden_pass(b, t, g, start, stop):
             moving = [x_first[:, b * P : (b + 1) * P], x_second[b][:]]
+            nc.tensor.matmul_mx(
+                out=h_acc[b][:, t, :],
+                lhsT=w_codes[g][t // 2][:, t % 2 * P : (t % 2 + 1) * P].bitcast(FP8X4),
+                lhsT_scale=w_scale[g][t // 2][:, t % 2 * P : (t % 2 + 1) * P],
+                rhs=moving[g].bitcast(FP8X4),
+                rhs_scale=x_scale[4 * g : P, b * P : (b + 1) * P],
+                start=start,
+                stop=stop,
+            )
+
+        def hidden_first(b):
+            for t in range(PACK):
+                hidden_pass(b, t, 0, t == 0, False)
+
+        def hidden_second(b):
+            for t in range(PACK):
+                hidden_pass(b, t, 1, False, t == PACK - 1)
+
+        def hidden_both(b):
             for t in range(PACK):
                 for g in range(PASSES):
-                    nc.tensor.matmul_mx(
-                        out=h_acc[:, t, :],
-                        lhsT=w_codes[g][:, t * P : (t + 1) * P].bitcast(FP8X4),
-                        lhsT_scale=w_scale[g][:, t * P : (t + 1) * P],
-                        rhs=moving[g].bitcast(FP8X4),
-                        rhs_scale=x_scale[4 * g : P, b * P : (b + 1) * P],
-                        start=(g == 0),
-                        stop=(g == PASSES - 1),
-                    )
-            if b in RELU_ON_VECTOR:
-                nc.vector.tensor_scalar_max(h_grouped[b][:], h_acc[:].rearrange("p t n -> p n t"), 0.0)
-            else:
-                nc.scalar.activation(h_grouped[b][:], h_acc[:].rearrange("p t n -> p n t"), ACT.Relu)
+                    hidden_pass(b, t, g, g == 0, g == PASSES - 1)
+
+        def rectify(b):
+            nc.scalar.activation(h_grouped[b][:], h_acc[b][:].rearrange("p t n -> p n t"), ACT.Relu)
 
         def quantize_h(b):
             nc.vector.quantize_mx(
@@ -163,9 +170,6 @@ def tile_picked_yhawem_log_p_kernel(
         def decayed_score(b):
             nc.vector.scalar_tensor_tensor(partial[b][:], y_acc[b][:], 0.0, decay[b][:], ALU.max, ALU.mult)
 
-        def mask(b):
-            nc.gpsimd.tensor_tensor(partial[b][:], decay[b][:], before_sb[b][:], ALU.mult)
-
         def finish(b, gg, total):
             lam = tile([P, 1], F32, f"lam{b}")
             nc.vector.tensor_scalar(lam[:], total[:], mu_sb[:, b : b + 1], 1.0 / 50.0, ALU.add, ALU.mult)
@@ -175,7 +179,7 @@ def tile_picked_yhawem_log_p_kernel(
             for c in range(STORE_PARTS[b]):
                 cols = slice(c * width, (c + 1) * width)
                 result = tile([P, width], F32, f"result{b}_{c}")
-                nc.scalar.activation(result[:], gg[:, cols], ACT.Ln, bias=0.05, scale=factor[:])
+                nc.scalar.activation(result[:], gg[:, cols], ACT.Ln, bias=floor[:], scale=factor[:])
                 nc.sync.dma_start(out[b * P : (b + 1) * P, cols], result[:])
 
         def share(b):
@@ -184,83 +188,57 @@ def tile_picked_yhawem_log_p_kernel(
             nc.vector.scalar_tensor_tensor(gg[:], partial[b][:], 1.0, before_sb[b][:], ALU.mult, ALU.mult, accum_out=total[:])
             finish(b, gg, total)
 
-        def share_masked(b):
-            gg = tile([P, V], F32, f"gg{b}")
-            total = tile([P, 1], F32, f"total{b}")
-            nc.vector.scalar_tensor_tensor(gg[:], y_acc[b][:], 0.0, partial[b][:], ALU.max, ALU.mult, accum_out=total[:])
-            finish(b, gg, total)
+        def stamp(i, ap):
+            nc.gpsimd.tensor_copy(clock[:, i : i + 1], ap.bitcast(U32))
 
-        nc.vector.memset(x_scale_table[:].bitcast(I32), 0)
-        nc.gpsimd.memset(e_scale_table[:].bitcast(I32), 0)
-        nc.vector.memset(mu_rows[:], 0.0)
-        nc.sync.dma_start(x_list[:], offs)
-        nc.sync.dma_start(e_list[:], past)
-        for q in range(4):
-            nc.scalar.dma_start(
-                x_scale_table[32 * q : 32 * q + 4 * PASSES, :].bitcast(I32),
-                x_scales[:, 4 * q : 4 * q + 4, :].bitcast(I32),
-            )
-        load_w(0)
+        nc.gpsimd.memset(x_scale_table[:].bitcast(I32), 0)
+        nc.vector.memset(e_scale_table[:].bitcast(I32), 0)
+        nc.gpsimd.memset(ones[:], 1.0)
+        nc.scalar.activation(floor[:], ones[:], ACT.Copy, scale=0.05)
+        nc.gpsimd.memset(mu_rows[:], 0.0)
         load_x(0)
-        load_w_half(0)
-        nc.sync.dma_start(mu_rows[:BLOCKS, :], mu.rearrange("(b p) o -> b (p o)", p=P))
+        nc.sync.dma_start(x_list[:], offs)
+        load_x_scales(nc.sync)
+        load_w(0)
+        nc.sync.dma_start(e_list[:], past)
+        load_e_scales(nc.sync)
+        load_w(1)
+        load_x(1)
+        load_e()
+        load_mu()
+        for b in range(BLOCKS):
+            load_ago(b)
+        for b in range(BLOCKS):
+            load_before(b)
         make_identity(nc, identity[:])
         mu_turned = psum.tile([P, P], F32, name="mu_turned", tag="y_acc3")
         nc.tensor.transpose(mu_turned[:], mu_rows[:], identity[:])
         nc.vector.tensor_copy(mu_sb[:], mu_turned[:, :BLOCKS])
-        spare = psum.tile([P, V], F32, name="spare", tag="y_acc0")
         y_acc = [psum.tile([P, V], F32, name=f"y_acc{b}", tag=f"y_acc{b}") for b in range(BLOCKS)]
-        load_w_half(1)
-        load_x(1)
-        for q in range(4):
-            nc.sync.dma_start(
-                e_scale_table[32 * q : 32 * q + 4, :].bitcast(I32),
-                e_scales[0, 4 * q : 4 * q + 4, :].bitcast(I32),
-            )
-        load_ago(0)
-        nc.sync.dma_start(e_table[:].bitcast(I32), e_words[0].rearrange("p n t -> p (n t)").bitcast(I32))
-        load_ago(1)
-        load_ago(2)
-        load_ago(3)
-        load_before(0)
-        load_before(1)
-        load_before(2)
-        load_before(3)
 
         nc.vector.tensor_copy(x_scale[:], x_scale_table[:].indirect(x_list[:]))
-        cast_w(0)
         nc.vector.tensor_copy(x_first[:], x_table[0][:].indirect(x_list[:]))
-        quantize_w(0)
-        warm(3)
-        cast_w(1)
-        quantize_w(1)
-        gather_x(0)
-        hidden(0)
-        gather_x(1)
-        hidden(1)
-        gather_x(2)
-        hidden(2)
-        gather_x(3)
-        hidden(3)
         nc.vector.tensor_copy(e_scale[:], e_scale_table[:].indirect(e_list[:]))
+        cast_w(0, 0, True)
+        cast_w(0, 1, False)
+        quantize_w(0, 0)
+        quantize_w(0, 1)
+        for b in range(BLOCKS):
+            hidden_first(b)
+        cast_w(1, 0, True)
+        cast_w(1, 1, False)
+        quantize_w(1, 1)
+        quantize_w(1, 0)
+        for b in range(BLOCKS):
+            gather_x(b)
+            hidden_second(b)
+            rectify(b)
         nc.vector.tensor_copy(e_codes[:], e_table[:].indirect(e_list[:]))
-        quantize_h(0)
-        score(0)
-        quantize_h(1)
-        score(1)
-        quantize_h(2)
-        score(2)
-        quantize_h(3)
-        score(3)
-        decay_of(0)
-        decay_of(1)
-        decay_of(2)
-        decay_of(3)
-        decayed_score(0)
-        share(0)
-        decayed_score(1)
-        share(1)
-        decayed_score(2)
-        share(2)
-        decayed_score(3)
-        share(3)
+        for b in range(BLOCKS):
+            quantize_h(b)
+            score(b)
+        for b in range(BLOCKS):
+            decay_of(b)
+        for b in range(BLOCKS):
+            decayed_score(b)
+            share(b)

@@ -23,6 +23,12 @@ PASSES = K // K_PASS
 BLOCKS = S // P
 LIST_ROWS = 16
 STORE_PARTS = [1,1,1,2]
+E_ROW = 8
+H_GROUPS = [[0,1],[2,3]]
+T_ORDER = [2, 3, 0, 1]
+RELU_ON_VECTOR = []
+HELD = []
+PARTIAL_SLOT = [0,1,2,2]
 EARLY_H = 0
 
 
@@ -32,6 +38,7 @@ def tile_picked_yhawem_log_p_kernel(
     nc = tc.nc
     with ExitStack() as ctx:
         keep = ctx.enter_context(tc.tile_pool(name="keep", bufs=1))
+        reuse = ctx.enter_context(tc.tile_pool(name="reuse", bufs=1))
         psum = ctx.enter_context(tc.psum_pool(name="psum", bufs=1))
 
         def tile(shape, dtype, name, tag=None):
@@ -42,26 +49,36 @@ def tile_picked_yhawem_log_p_kernel(
         x_scale_table = tile([P, T], U8, "x_scale_table")
         e_scale_table = tile([P, W], U8, "e_scale_table")
         x_table = [tile([P, T], U32, f"x_table{g}") for g in range(PASSES)]
-        e_table = tile([P, W], U32, "e_table")
+        e_table = reuse.tile([P, W], U32, name="e_table", offset=0, align_bytes=64)
         w_raw = [tile([P, PACK, H], F32, f"w_raw{g}") for g in range(PASSES)]
         mu_sb = tile([P, BLOCKS], F32, "mu_sb")
         ago_sb = [tile([P, V], F32, f"ago{b}") for b in range(BLOCKS)]
         before_sb = [tile([P, V], F32, f"before{b}") for b in range(BLOCKS)]
         x_scale = tile([P, S], U8, "x_scale")
-        e_scale = tile([P, V], U8, "e_scale")
         x_first = tile([P, S], U32, "x_first")
-        x_second = [tile([P, P], U32, f"x_second{b}") for b in range(BLOCKS)]
         e_codes = tile([P, V], U32, "e_codes")
         w_grouped = [[tile([P, 2, P, PACK], BF16, f"w_grouped{g}_{u}") for u in range(2)] for g in range(PASSES)]
+        x_head = tile([P, P], U32, "x_head")
+        x_rest = tile([P, BLOCKS - 1, P], U32, "x_rest", tag="w_grouped1_0")
+        x_second = [x_head[:]] + [x_rest[:, b, :] for b in range(BLOCKS - 1)]
+        e_scale = tile([P, V], U8, "e_scale")
         w_codes = [[tile([P, 2 * P], U32, f"w_codes{g}_{u}") for u in range(2)] for g in range(PASSES)]
         w_scale = [[tile([P, 2 * P], U8, f"w_scale{g}_{u}") for u in range(2)] for g in range(PASSES)]
-        h_late = tile([P, BLOCKS, P], U32, "h_late", tag="e_table")
-        h_early = tile([P, BLOCKS, P], U32, "h_early")
-        h_codes = [(h_early if b < EARLY_H else h_late)[:, b, :] for b in range(BLOCKS)]
-        h_grouped = [tile([P, P, PACK], BF16, f"h_grouped{b}") for b in range(BLOCKS)]
-        h_scale = [tile([P, P], U8, f"h_scale{b}") for b in range(BLOCKS)]
+        h_grouped = [
+            reuse.tile([P, len(bs), P, PACK], BF16, name=f"h_grouped{i}", offset=4 * S + 1024 * bs[0], align_bytes=64)
+            if bs[0] in RELU_ON_VECTOR
+            else tile([P, len(bs), P, PACK], BF16, f"h_grouped{i}")
+            for i, bs in enumerate(H_GROUPS)
+        ]
+        h_scale = [tile([P, len(bs) * P], U8, f"h_scale{i}") for i, bs in enumerate(H_GROUPS)]
+        h_late = reuse.tile([P, S], U32, name="h_late", offset=0, align_bytes=64)
+        h_early = tile([P, S], U32, "h_early")
+        place = {b: (i, bs.index(b)) for i, bs in enumerate(H_GROUPS) for b in bs}
+
+        def h_codes(first, count):
+            return (h_early if first < EARLY_H else h_late)[:, first * P : (first + count) * P]
         decay = [tile([P, V], F32, f"decay{b}") for b in range(BLOCKS)]
-        partial = [tile([P, V], F32, f"partial{b}") for b in range(BLOCKS)]
+        partial = {}
         mu_rows = tile([P, P], F32, "mu_rows")
         identity = tile([P, P], F32, "identity")
         ones = tile([P, 1], F32, "ones")
@@ -89,10 +106,10 @@ def tile_picked_yhawem_log_p_kernel(
                 )
 
         def load_e_scales(queue):
-            for q in range(4):
+            for r in range(4):
                 queue.dma_start(
-                    e_scale_table[32 * q : 32 * q + 4, :].bitcast(I32),
-                    e_scales[0, 4 * q : 4 * q + 4, :].bitcast(I32),
+                    e_scale_table[E_ROW + r : P : 32, :].bitcast(I32),
+                    e_scales[0, r : 16 : 4, :].bitcast(I32),
                 )
 
         def load_e():
@@ -116,12 +133,12 @@ def tile_picked_yhawem_log_p_kernel(
 
         def gather_x(b):
             entries = x_list[:, b * P // LIST_ROWS : (b + 1) * P // LIST_ROWS]
-            nc.vector.tensor_copy(x_second[b][:], x_table[1][:].indirect(entries))
+            nc.vector.tensor_copy(x_second[b], x_table[1][:].indirect(entries))
 
         h_acc = [psum.tile([P, PACK, P], F32, name=f"h_acc{b}") for b in range(BLOCKS)]
 
         def hidden_pass(b, t, g, start, stop):
-            moving = [x_first[:, b * P : (b + 1) * P], x_second[b][:]]
+            moving = [x_first[:, b * P : (b + 1) * P], x_second[b]]
             nc.tensor.matmul_mx(
                 out=h_acc[b][:, t, :],
                 lhsT=w_codes[g][t // 2][:, t % 2 * P : (t % 2 + 1) * P].bitcast(FP8X4),
@@ -133,33 +150,47 @@ def tile_picked_yhawem_log_p_kernel(
             )
 
         def hidden_first(b):
-            for t in range(PACK):
-                hidden_pass(b, t, 0, t == 0, False)
+            for t in T_ORDER:
+                hidden_pass(b, t, 0, t == T_ORDER[0], False)
 
         def hidden_second(b):
-            for t in range(PACK):
-                hidden_pass(b, t, 1, False, t == PACK - 1)
+            for t in T_ORDER:
+                hidden_pass(b, t, 1, False, t == T_ORDER[-1])
 
-        def hidden_both(b):
-            for t in range(PACK):
-                for g in range(PASSES):
-                    hidden_pass(b, t, g, g == 0, g == PASSES - 1)
+        def warm(n):
+            spare = psum.tile([P, V], F32, name="spare", tag="y_acc0")
+            for r in range(n):
+                nc.tensor.matmul_mx(
+                    out=spare[:],
+                    lhsT=x_first[:, :P].bitcast(FP8X4),
+                    lhsT_scale=x_scale[:, :P],
+                    rhs=x_first[:].bitcast(FP8X4),
+                    rhs_scale=x_scale[:],
+                    start=True,
+                    stop=True,
+                )
 
         def rectify(b):
-            nc.scalar.activation(h_grouped[b][:], h_acc[b][:].rearrange("p t n -> p n t"), ACT.Relu)
+            dst = h_grouped[place[b][0]][:, place[b][1]]
+            src = h_acc[b][:].rearrange("p t n -> p n t")
+            if b in RELU_ON_VECTOR:
+                nc.vector.tensor_scalar_max(dst, src, 0.0)
+            else:
+                nc.scalar.activation(dst, src, ACT.Relu)
 
-        def quantize_h(b):
+        def quantize_h(i):
+            bs = H_GROUPS[i]
             nc.vector.quantize_mx(
-                h_codes[b].bitcast(FP8X4), h_scale[b][:], h_grouped[b][:].rearrange("p n t -> p (n t)")
+                h_codes(bs[0], len(bs)).bitcast(FP8X4), h_scale[i][:], h_grouped[i][:].rearrange("p b n t -> p (b n t)")
             )
 
         def score(b):
             nc.tensor.matmul_mx(
                 out=y_acc[b][:],
-                lhsT=h_codes[b].bitcast(FP8X4),
-                lhsT_scale=h_scale[b][:],
+                lhsT=h_codes(b, 1).bitcast(FP8X4),
+                lhsT_scale=h_scale[place[b][0]][:, place[b][1] * P : (place[b][1] + 1) * P],
                 rhs=e_codes[:].bitcast(FP8X4),
-                rhs_scale=e_scale[:],
+                rhs_scale=e_scale[E_ROW:P, :],
                 start=True,
                 stop=True,
             )
@@ -168,6 +199,7 @@ def tile_picked_yhawem_log_p_kernel(
             nc.scalar.activation(decay[u][:], ago_sb[u][:], ACT.Exp, scale=-0.7)
 
         def decayed_score(b):
+            partial[b] = tile([P, V], F32, f"partial{b}", tag=f"partial{PARTIAL_SLOT[b]}")
             nc.vector.scalar_tensor_tensor(partial[b][:], y_acc[b][:], 0.0, decay[b][:], ALU.max, ALU.mult)
 
         def finish(b, gg, total):
@@ -184,7 +216,7 @@ def tile_picked_yhawem_log_p_kernel(
 
         def share(b):
             gg = tile([P, V], F32, f"gg{b}")
-            total = tile([P, 1], F32, f"total{b}")
+            total = tile([P, 1], F32, f"total{b}", tag=f"lam{b - 1}" if b in HELD else None)
             nc.vector.scalar_tensor_tensor(gg[:], partial[b][:], 1.0, before_sb[b][:], ALU.mult, ALU.mult, accum_out=total[:])
             finish(b, gg, total)
 
@@ -221,8 +253,8 @@ def tile_picked_yhawem_log_p_kernel(
         nc.vector.tensor_copy(e_scale[:], e_scale_table[:].indirect(e_list[:]))
         cast_w(0, 0, True)
         cast_w(0, 1, False)
-        quantize_w(0, 0)
         quantize_w(0, 1)
+        quantize_w(0, 0)
         for b in range(BLOCKS):
             hidden_first(b)
         cast_w(1, 0, True)
@@ -232,11 +264,15 @@ def tile_picked_yhawem_log_p_kernel(
         for b in range(BLOCKS):
             gather_x(b)
             hidden_second(b)
-            rectify(b)
+            if b not in RELU_ON_VECTOR:
+                rectify(b)
         nc.vector.tensor_copy(e_codes[:], e_table[:].indirect(e_list[:]))
-        for b in range(BLOCKS):
-            quantize_h(b)
-            score(b)
+        for i, bs in enumerate(H_GROUPS):
+            if bs[0] in RELU_ON_VECTOR:
+                rectify(bs[0])
+            quantize_h(i)
+            for b in bs:
+                score(b)
         for b in range(BLOCKS):
             decay_of(b)
         for b in range(BLOCKS):

@@ -22,13 +22,13 @@ K_PASS = P * PACK
 PASSES = K // K_PASS
 BLOCKS = S // P
 LIST_ROWS = 16
-STORE_PARTS = [1,1,1,2]
+STORE_PARTS = [1,1,2,1]
 E_ROW = 8
-H_GROUPS = [[0,1],[2,3]]
+H_GROUPS = [[0,1],[2],[3]]
 T_ORDER = [2, 3, 0, 1]
-RELU_ON_VECTOR = []
+RELU_ON_VECTOR = [3]
 HELD = []
-PARTIAL_SLOT = [0,1,2,2]
+PARTIAL_SLOT = [0,1,2,3]
 EARLY_H = 0
 
 
@@ -215,9 +215,19 @@ def tile_picked_yhawem_log_p_kernel(
                 nc.sync.dma_start(out[b * P : (b + 1) * P, cols], result[:])
 
         def share(b):
-            gg = tile([P, V], F32, f"gg{b}")
+            gg = tile([P, V], F32, f"gg{b}", tag="decay2" if b == 0 else None)
             total = tile([P, 1], F32, f"total{b}", tag=f"lam{b - 1}" if b in HELD else None)
             nc.vector.scalar_tensor_tensor(gg[:], partial[b][:], 1.0, before_sb[b][:], ALU.mult, ALU.mult, accum_out=total[:])
+            finish(b, gg, total)
+
+        def mask(b):
+            partial[b] = tile([P, V], F32, f"partial{b}")
+            nc.gpsimd.tensor_tensor(partial[b][:], decay[b][:], before_sb[b][:], ALU.mult)
+
+        def share_masked(b):
+            gg = tile([P, V], F32, f"gg{b}")
+            total = tile([P, 1], F32, f"total{b}")
+            nc.vector.scalar_tensor_tensor(gg[:], y_acc[b][:], 0.0, partial[b][:], ALU.max, ALU.mult, accum_out=total[:])
             finish(b, gg, total)
 
         def stamp(i, ap):
@@ -238,9 +248,9 @@ def tile_picked_yhawem_log_p_kernel(
         load_x(1)
         load_e()
         load_mu()
-        for b in range(BLOCKS):
+        for b in (0, 3, 1, 2):
             load_ago(b)
-        for b in range(BLOCKS):
+        for b in (3, 0, 1, 2):
             load_before(b)
         make_identity(nc, identity[:])
         mu_turned = psum.tile([P, P], F32, name="mu_turned", tag="y_acc3")
@@ -273,8 +283,13 @@ def tile_picked_yhawem_log_p_kernel(
             quantize_h(i)
             for b in bs:
                 score(b)
-        for b in range(BLOCKS):
+        for b in (0, 3, 1, 2):
             decay_of(b)
-        for b in range(BLOCKS):
-            decayed_score(b)
-            share(b)
+        mask(3)
+        decayed_score(0)
+        decayed_score(1)
+        decayed_score(2)
+        share(0)
+        share_masked(3)
+        share(1)
+        share(2)

@@ -18,18 +18,20 @@ ACT = mybir.ActivationFunctionType
 
 P = 128
 PACK = 4
+QUADRANT = 32
 K_PASS = P * PACK
 PASSES = K // K_PASS
 BLOCKS = S // P
 LIST_ROWS = 16
-STORE_PARTS = [1,1,2,1]
-E_ROW = 8
-H_GROUPS = [[0,1],[2],[3]]
-T_ORDER = [2, 3, 0, 1]
-RELU_ON_VECTOR = [3]
-HELD = []
-PARTIAL_SLOT = [0,1,2,3]
-EARLY_H = 0
+PAIR = 2
+SCALAR_PAIR, VECTOR_PAIR = 0, 1
+TILE_ORDER = [2, 3, 0, 1]
+E_FIRST = PACK * PASSES
+H_GROUPS = [[0, 1], [2], [3]]
+LAST = BLOCKS - 1
+AGO_ORDER = [0, LAST, 1, 2]
+BEFORE_ORDER = [LAST, 0, 1, 2]
+STORE_PARTS = [1, 1, 2, 1]
 
 
 def tile_picked_yhawem_log_p_kernel(
@@ -57,33 +59,30 @@ def tile_picked_yhawem_log_p_kernel(
         x_scale = tile([P, S], U8, "x_scale")
         x_first = tile([P, S], U32, "x_first")
         e_codes = tile([P, V], U32, "e_codes")
-        w_grouped = [[tile([P, 2, P, PACK], BF16, f"w_grouped{g}_{u}") for u in range(2)] for g in range(PASSES)]
+        w_grouped = [[tile([P, PAIR, P, PACK], BF16, f"w_grouped{g}_{u}") for u in range(PACK // PAIR)] for g in range(PASSES)]
         x_head = tile([P, P], U32, "x_head")
-        x_rest = tile([P, BLOCKS - 1, P], U32, "x_rest", tag="w_grouped1_0")
+        x_rest = tile([P, BLOCKS - 1, P], U32, "x_rest", tag=f"w_grouped1_{SCALAR_PAIR}")
         x_second = [x_head[:]] + [x_rest[:, b, :] for b in range(BLOCKS - 1)]
         e_scale = tile([P, V], U8, "e_scale")
-        w_codes = [[tile([P, 2 * P], U32, f"w_codes{g}_{u}") for u in range(2)] for g in range(PASSES)]
-        w_scale = [[tile([P, 2 * P], U8, f"w_scale{g}_{u}") for u in range(2)] for g in range(PASSES)]
+        w_codes = [[tile([P, PAIR * P], U32, f"w_codes{g}_{u}") for u in range(PACK // PAIR)] for g in range(PASSES)]
+        w_scale = [[tile([P, PAIR * P], U8, f"w_scale{g}_{u}") for u in range(PACK // PAIR)] for g in range(PASSES)]
+        code_bytes = PACK * S
         h_grouped = [
-            reuse.tile([P, len(bs), P, PACK], BF16, name=f"h_grouped{i}", offset=4 * S + 1024 * bs[0], align_bytes=64)
-            if bs[0] in RELU_ON_VECTOR
+            reuse.tile([P, len(bs), P, PACK], BF16, name=f"h_grouped{i}", offset=code_bytes, align_bytes=64)
+            if bs == [LAST]
             else tile([P, len(bs), P, PACK], BF16, f"h_grouped{i}")
             for i, bs in enumerate(H_GROUPS)
         ]
         h_scale = [tile([P, len(bs) * P], U8, f"h_scale{i}") for i, bs in enumerate(H_GROUPS)]
-        h_late = reuse.tile([P, S], U32, name="h_late", offset=0, align_bytes=64)
-        h_early = tile([P, S], U32, "h_early")
+        h_codes = reuse.tile([P, S], U32, name="h_codes", offset=0, align_bytes=64)
         place = {b: (i, bs.index(b)) for i, bs in enumerate(H_GROUPS) for b in bs}
-
-        def h_codes(first, count):
-            return (h_early if first < EARLY_H else h_late)[:, first * P : (first + count) * P]
         decay = [tile([P, V], F32, f"decay{b}") for b in range(BLOCKS)]
-        partial = {}
+        partial = [tile([P, V], F32, f"partial{b}") for b in range(BLOCKS)]
         mu_rows = tile([P, P], F32, "mu_rows")
         identity = tile([P, P], F32, "identity")
         ones = tile([P, 1], F32, "ones")
         floor = tile([P, 1], F32, "floor")
-        clock = tile([P, 8], U32, "clock")
+        h_acc = [psum.tile([P, PACK, P], F32, name=f"h_acc{b}") for b in range(BLOCKS)]
 
         def load_x(g):
             nc.sync.dma_start(x_table[g][:].bitcast(I32), x_words[g].rearrange("p n t -> p (n t)").bitcast(I32))
@@ -92,117 +91,91 @@ def tile_picked_yhawem_log_p_kernel(
             rows = slice(g * K_PASS, (g + 1) * K_PASS)
             nc.sync.dma_start(w_raw[g][:], w1[rows, :].rearrange("(p j) c -> p j c", j=PACK))
 
-        def load_ago(u):
-            nc.sync.dma_start(ago_sb[u][:], ago[u * P : (u + 1) * P, :])
-
-        def load_before(b):
-            nc.sync.dma_start(before_sb[b][:], before[b * P : (b + 1) * P, :])
-
-        def load_x_scales(queue):
-            for q in range(4):
-                queue.dma_start(
-                    x_scale_table[32 * q : 32 * q + 4 * PASSES, :].bitcast(I32),
-                    x_scales[:, 4 * q : 4 * q + 4, :].bitcast(I32),
+        def load_x_scales():
+            for q in range(P // QUADRANT):
+                nc.sync.dma_start(
+                    x_scale_table[QUADRANT * q : QUADRANT * q + PACK * PASSES, :].bitcast(I32),
+                    x_scales[:, PACK * q : PACK * (q + 1), :].bitcast(I32),
                 )
 
-        def load_e_scales(queue):
-            for r in range(4):
-                queue.dma_start(
-                    e_scale_table[E_ROW + r : P : 32, :].bitcast(I32),
-                    e_scales[0, r : 16 : 4, :].bitcast(I32),
+        def load_e_scales():
+            for r in range(PACK):
+                nc.sync.dma_start(
+                    e_scale_table[E_FIRST + r : P : QUADRANT, :].bitcast(I32),
+                    e_scales[0, r : PACK * P // QUADRANT : PACK, :].bitcast(I32),
                 )
 
-        def load_e():
-            nc.sync.dma_start(e_table[:].bitcast(I32), e_words[0].rearrange("p n t -> p (n t)").bitcast(I32))
-
-        def load_mu():
-            nc.sync.dma_start(mu_rows[:BLOCKS, :], mu.rearrange("(b p) o -> b (p o)", p=P))
-
-        def cast_w(g, u, on_scalar):
+        def round_w(g, u):
             dst = w_grouped[g][u][:].rearrange("p t m j -> p m j t")
-            src = w_raw[g][:].rearrange("p j (m t) -> p m j t", t=PACK)[:, :, :, 2 * u : 2 * u + 2]
-            if on_scalar:
+            src = w_raw[g][:].rearrange("p j (m t) -> p m j t", t=PACK)[:, :, :, PAIR * u : PAIR * (u + 1)]
+            if u == SCALAR_PAIR:
                 nc.scalar.copy(dst, src)
             else:
                 nc.vector.tensor_copy(dst, src)
 
-        def quantize_w(g, u):
-            nc.vector.quantize_mx(
-                w_codes[g][u][:].bitcast(FP8X4), w_scale[g][u][:], w_grouped[g][u][:].rearrange("p t m j -> p (t m j)")
-            )
+        def quantize_w(g):
+            for u in (SCALAR_PAIR, VECTOR_PAIR):
+                round_w(g, u)
+            for u in (VECTOR_PAIR, SCALAR_PAIR):
+                nc.vector.quantize_mx(
+                    w_codes[g][u][:].bitcast(FP8X4), w_scale[g][u][:], w_grouped[g][u][:].rearrange("p t m j -> p (t m j)")
+                )
 
-        def gather_x(b):
+        def gather_x_second(b):
             entries = x_list[:, b * P // LIST_ROWS : (b + 1) * P // LIST_ROWS]
             nc.vector.tensor_copy(x_second[b], x_table[1][:].indirect(entries))
 
-        h_acc = [psum.tile([P, PACK, P], F32, name=f"h_acc{b}") for b in range(BLOCKS)]
-
-        def hidden_pass(b, t, g, start, stop):
-            moving = [x_first[:, b * P : (b + 1) * P], x_second[b]]
-            nc.tensor.matmul_mx(
-                out=h_acc[b][:, t, :],
-                lhsT=w_codes[g][t // 2][:, t % 2 * P : (t % 2 + 1) * P].bitcast(FP8X4),
-                lhsT_scale=w_scale[g][t // 2][:, t % 2 * P : (t % 2 + 1) * P],
-                rhs=moving[g].bitcast(FP8X4),
-                rhs_scale=x_scale[4 * g : P, b * P : (b + 1) * P],
-                start=start,
-                stop=stop,
-            )
-
-        def hidden_first(b):
-            for t in T_ORDER:
-                hidden_pass(b, t, 0, t == T_ORDER[0], False)
-
-        def hidden_second(b):
-            for t in T_ORDER:
-                hidden_pass(b, t, 1, False, t == T_ORDER[-1])
-
-        def warm(n):
-            spare = psum.tile([P, V], F32, name="spare", tag="y_acc0")
-            for r in range(n):
+        def hidden(b, g):
+            events = slice(b * P, (b + 1) * P)
+            moving = x_first[:, events] if g == 0 else x_second[b]
+            for t in TILE_ORDER:
+                cols = slice(t % PAIR * P, (t % PAIR + 1) * P)
                 nc.tensor.matmul_mx(
-                    out=spare[:],
-                    lhsT=x_first[:, :P].bitcast(FP8X4),
-                    lhsT_scale=x_scale[:, :P],
-                    rhs=x_first[:].bitcast(FP8X4),
-                    rhs_scale=x_scale[:],
-                    start=True,
-                    stop=True,
+                    out=h_acc[b][:, t, :],
+                    lhsT=w_codes[g][t // PAIR][:, cols].bitcast(FP8X4),
+                    lhsT_scale=w_scale[g][t // PAIR][:, cols],
+                    rhs=moving.bitcast(FP8X4),
+                    rhs_scale=x_scale[PACK * g : P, events],
+                    start=g == 0 and t == TILE_ORDER[0],
+                    stop=g == PASSES - 1 and t == TILE_ORDER[-1],
                 )
 
         def rectify(b):
-            dst = h_grouped[place[b][0]][:, place[b][1]]
+            group, slot = place[b]
+            dst = h_grouped[group][:, slot]
             src = h_acc[b][:].rearrange("p t n -> p n t")
-            if b in RELU_ON_VECTOR:
+            if b == LAST:
                 nc.vector.tensor_scalar_max(dst, src, 0.0)
             else:
                 nc.scalar.activation(dst, src, ACT.Relu)
 
-        def quantize_h(i):
-            bs = H_GROUPS[i]
+        def quantize_h(group):
+            bs = H_GROUPS[group]
             nc.vector.quantize_mx(
-                h_codes(bs[0], len(bs)).bitcast(FP8X4), h_scale[i][:], h_grouped[i][:].rearrange("p b n t -> p (b n t)")
+                h_codes[:, bs[0] * P : (bs[-1] + 1) * P].bitcast(FP8X4),
+                h_scale[group][:],
+                h_grouped[group][:].rearrange("p b n t -> p (b n t)"),
             )
 
         def score(b):
+            group, slot = place[b]
             nc.tensor.matmul_mx(
                 out=y_acc[b][:],
-                lhsT=h_codes(b, 1).bitcast(FP8X4),
-                lhsT_scale=h_scale[place[b][0]][:, place[b][1] * P : (place[b][1] + 1) * P],
+                lhsT=h_codes[:, b * P : (b + 1) * P].bitcast(FP8X4),
+                lhsT_scale=h_scale[group][:, slot * P : (slot + 1) * P],
                 rhs=e_codes[:].bitcast(FP8X4),
-                rhs_scale=e_scale[E_ROW:P, :],
+                rhs_scale=e_scale[E_FIRST:P, :],
                 start=True,
                 stop=True,
             )
 
-        def decay_of(u):
-            nc.scalar.activation(decay[u][:], ago_sb[u][:], ACT.Exp, scale=-0.7)
-
-        def decayed_score(b):
-            partial[b] = tile([P, V], F32, f"partial{b}", tag=f"partial{PARTIAL_SLOT[b]}")
-            nc.vector.scalar_tensor_tensor(partial[b][:], y_acc[b][:], 0.0, decay[b][:], ALU.max, ALU.mult)
-
-        def finish(b, gg, total):
+        def share(b):
+            gg = tile([P, V], F32, f"gg{b}", tag=f"decay{AGO_ORDER[-1]}" if b == 0 else None)
+            total = tile([P, 1], F32, f"total{b}")
+            if b == LAST:
+                nc.vector.scalar_tensor_tensor(gg[:], y_acc[b][:], 0.0, partial[b][:], ALU.max, ALU.mult, accum_out=total[:])
+            else:
+                nc.vector.scalar_tensor_tensor(gg[:], partial[b][:], 1.0, before_sb[b][:], ALU.mult, ALU.mult, accum_out=total[:])
             lam = tile([P, 1], F32, f"lam{b}")
             nc.vector.tensor_scalar(lam[:], total[:], mu_sb[:, b : b + 1], 1.0 / 50.0, ALU.add, ALU.mult)
             factor = tile([P, 1], F32, f"factor{b}")
@@ -214,46 +187,28 @@ def tile_picked_yhawem_log_p_kernel(
                 nc.scalar.activation(result[:], gg[:, cols], ACT.Ln, bias=floor[:], scale=factor[:])
                 nc.sync.dma_start(out[b * P : (b + 1) * P, cols], result[:])
 
-        def share(b):
-            gg = tile([P, V], F32, f"gg{b}", tag="decay2" if b == 0 else None)
-            total = tile([P, 1], F32, f"total{b}", tag=f"lam{b - 1}" if b in HELD else None)
-            nc.vector.scalar_tensor_tensor(gg[:], partial[b][:], 1.0, before_sb[b][:], ALU.mult, ALU.mult, accum_out=total[:])
-            finish(b, gg, total)
-
-        def mask(b):
-            partial[b] = tile([P, V], F32, f"partial{b}")
-            nc.gpsimd.tensor_tensor(partial[b][:], decay[b][:], before_sb[b][:], ALU.mult)
-
-        def share_masked(b):
-            gg = tile([P, V], F32, f"gg{b}")
-            total = tile([P, 1], F32, f"total{b}")
-            nc.vector.scalar_tensor_tensor(gg[:], y_acc[b][:], 0.0, partial[b][:], ALU.max, ALU.mult, accum_out=total[:])
-            finish(b, gg, total)
-
-        def stamp(i, ap):
-            nc.gpsimd.tensor_copy(clock[:, i : i + 1], ap.bitcast(U32))
-
         nc.gpsimd.memset(x_scale_table[:].bitcast(I32), 0)
         nc.vector.memset(e_scale_table[:].bitcast(I32), 0)
         nc.gpsimd.memset(ones[:], 1.0)
         nc.scalar.activation(floor[:], ones[:], ACT.Copy, scale=0.05)
         nc.gpsimd.memset(mu_rows[:], 0.0)
+
         load_x(0)
         nc.sync.dma_start(x_list[:], offs)
-        load_x_scales(nc.sync)
+        load_x_scales()
         load_w(0)
         nc.sync.dma_start(e_list[:], past)
-        load_e_scales(nc.sync)
+        load_e_scales()
         load_w(1)
         load_x(1)
-        load_e()
-        load_mu()
-        for b in (0, 3, 1, 2):
-            load_ago(b)
-        for b in (3, 0, 1, 2):
-            load_before(b)
+        nc.sync.dma_start(e_table[:].bitcast(I32), e_words[0].rearrange("p n t -> p (n t)").bitcast(I32))
+        nc.sync.dma_start(mu_rows[:BLOCKS, :], mu.rearrange("(b p) o -> b (p o)", p=P))
+        for b in AGO_ORDER:
+            nc.sync.dma_start(ago_sb[b][:], ago[b * P : (b + 1) * P, :])
+        for b in BEFORE_ORDER:
+            nc.sync.dma_start(before_sb[b][:], before[b * P : (b + 1) * P, :])
         make_identity(nc, identity[:])
-        mu_turned = psum.tile([P, P], F32, name="mu_turned", tag="y_acc3")
+        mu_turned = psum.tile([P, P], F32, name="mu_turned", tag=f"y_acc{LAST}")
         nc.tensor.transpose(mu_turned[:], mu_rows[:], identity[:])
         nc.vector.tensor_copy(mu_sb[:], mu_turned[:, :BLOCKS])
         y_acc = [psum.tile([P, V], F32, name=f"y_acc{b}", tag=f"y_acc{b}") for b in range(BLOCKS)]
@@ -261,35 +216,26 @@ def tile_picked_yhawem_log_p_kernel(
         nc.vector.tensor_copy(x_scale[:], x_scale_table[:].indirect(x_list[:]))
         nc.vector.tensor_copy(x_first[:], x_table[0][:].indirect(x_list[:]))
         nc.vector.tensor_copy(e_scale[:], e_scale_table[:].indirect(e_list[:]))
-        cast_w(0, 0, True)
-        cast_w(0, 1, False)
-        quantize_w(0, 1)
-        quantize_w(0, 0)
+        quantize_w(0)
         for b in range(BLOCKS):
-            hidden_first(b)
-        cast_w(1, 0, True)
-        cast_w(1, 1, False)
-        quantize_w(1, 1)
-        quantize_w(1, 0)
+            hidden(b, 0)
+        quantize_w(1)
         for b in range(BLOCKS):
-            gather_x(b)
-            hidden_second(b)
-            if b not in RELU_ON_VECTOR:
+            gather_x_second(b)
+            hidden(b, 1)
+            if b != LAST:
                 rectify(b)
         nc.vector.tensor_copy(e_codes[:], e_table[:].indirect(e_list[:]))
-        for i, bs in enumerate(H_GROUPS):
-            if bs[0] in RELU_ON_VECTOR:
-                rectify(bs[0])
-            quantize_h(i)
+        for group, bs in enumerate(H_GROUPS):
+            if bs == [LAST]:
+                rectify(LAST)
+            quantize_h(group)
             for b in bs:
                 score(b)
-        for b in (0, 3, 1, 2):
-            decay_of(b)
-        mask(3)
-        decayed_score(0)
-        decayed_score(1)
-        decayed_score(2)
-        share(0)
-        share_masked(3)
-        share(1)
-        share(2)
+        for b in AGO_ORDER:
+            nc.scalar.activation(decay[b][:], ago_sb[b][:], ACT.Exp, scale=-0.7)
+        nc.gpsimd.tensor_tensor(partial[LAST][:], decay[LAST][:], before_sb[LAST][:], ALU.mult)
+        for b in range(LAST):
+            nc.vector.scalar_tensor_tensor(partial[b][:], y_acc[b][:], 0.0, decay[b][:], ALU.max, ALU.mult)
+        for b in AGO_ORDER:
+            share(b)

@@ -25,9 +25,13 @@ BLOCKS = S // P
 LIST_ROWS = 16
 PAIR = 2
 SCALAR_PAIR, VECTOR_PAIR = 0, 1
-TILE_ORDER = [2, 3, 0, 1]
-E_FIRST = PACK * PASSES
+E_STEP = 8
 H_GROUPS = [[0, 1], [2], [3]]
+W_PARTS = [[0, 2], [2, 0]]
+ROUNDS = [
+    [(1, 0, P // 2, "vector"), (0, 0, P, "scalar"), (1, P // 2, P, "scalar")],
+    [(0, 0, P, "vector"), (1, 0, P, "scalar")],
+]
 LAST = BLOCKS - 1
 AGO_ORDER = [0, LAST, 1, 2]
 BEFORE_ORDER = [LAST, 0, 1, 2]
@@ -52,29 +56,35 @@ def tile_picked_yhawem_log_p_kernel(
         e_scale_table = tile([P, W], U8, "e_scale_table")
         x_table = [tile([P, T], U32, f"x_table{g}") for g in range(PASSES)]
         e_table = reuse.tile([P, W], U32, name="e_table", offset=0, align_bytes=64)
-        w_raw = [tile([P, PACK, H], F32, f"w_raw{g}") for g in range(PASSES)]
+        raw_bytes = PACK * H * 4
+        raw_start = W * 4
+        w_raw = [reuse.tile([P, PACK, H], F32, name=f"w_raw{g}", offset=raw_start + g * raw_bytes, align_bytes=64) for g in range(PASSES)]
         mu_sb = tile([P, BLOCKS], F32, "mu_sb")
-        ago_sb = [tile([P, V], F32, f"ago{b}") for b in range(BLOCKS)]
-        before_sb = [tile([P, V], F32, f"before{b}") for b in range(BLOCKS)]
+        ago_sb = [reuse.tile([P, V], F32, name=f"ago{b}", offset=raw_start + b * V * 4, align_bytes=64) for b in range(BLOCKS)]
+        before_sb = [
+            reuse.tile([P, V], F32, name=f"before{b}", offset=raw_start + raw_bytes + b * V * 4, align_bytes=64) for b in range(BLOCKS)
+        ]
         x_scale = tile([P, S], U8, "x_scale")
         x_first = tile([P, S], U32, "x_first")
         e_codes = tile([P, V], U32, "e_codes")
         w_grouped = [[tile([P, PAIR, P, PACK], BF16, f"w_grouped{g}_{u}") for u in range(PACK // PAIR)] for g in range(PASSES)]
         x_head = tile([P, P], U32, "x_head")
-        x_rest = tile([P, BLOCKS - 1, P], U32, "x_rest", tag=f"w_grouped1_{SCALAR_PAIR}")
+        x_rest = tile([P, BLOCKS - 1, P], U32, "x_rest", tag="w_grouped1_1")
         x_second = [x_head[:]] + [x_rest[:, b, :] for b in range(BLOCKS - 1)]
+        e_picked = tile([P, V], U8, "e_picked")
         e_scale = tile([P, V], U8, "e_scale")
         w_codes = [[tile([P, PAIR * P], U32, f"w_codes{g}_{u}") for u in range(PACK // PAIR)] for g in range(PASSES)]
         w_scale = [[tile([P, PAIR * P], U8, f"w_scale{g}_{u}") for u in range(PACK // PAIR)] for g in range(PASSES)]
-        code_bytes = PACK * S
         h_grouped = [
-            reuse.tile([P, len(bs), P, PACK], BF16, name=f"h_grouped{i}", offset=code_bytes, align_bytes=64)
+            reuse.tile([P, len(bs), P, PACK], BF16, name=f"h_grouped{i}", offset=S * 4, align_bytes=64)
             if bs == [LAST]
             else tile([P, len(bs), P, PACK], BF16, f"h_grouped{i}")
             for i, bs in enumerate(H_GROUPS)
         ]
         h_scale = [tile([P, len(bs) * P], U8, f"h_scale{i}") for i, bs in enumerate(H_GROUPS)]
-        h_codes = reuse.tile([P, S], U32, name="h_codes", offset=0, align_bytes=64)
+        h_codes = [
+            reuse.tile([P, len(bs) * P], U32, name=f"h_codes{i}", offset=bs[0] * P * 4, align_bytes=64) for i, bs in enumerate(H_GROUPS)
+        ]
         place = {b: (i, bs.index(b)) for i, bs in enumerate(H_GROUPS) for b in bs}
         decay = [tile([P, V], F32, f"decay{b}") for b in range(BLOCKS)]
         partial = [tile([P, V], F32, f"partial{b}") for b in range(BLOCKS)]
@@ -98,25 +108,22 @@ def tile_picked_yhawem_log_p_kernel(
                     x_scales[:, PACK * q : PACK * (q + 1), :].bitcast(I32),
                 )
 
-        def load_e_scales():
+        def move_e_scales():
             for r in range(PACK):
-                nc.sync.dma_start(
-                    e_scale_table[E_FIRST + r : P : QUADRANT, :].bitcast(I32),
-                    e_scales[0, r : PACK * P // QUADRANT : PACK, :].bitcast(I32),
-                )
+                nc.sync.dma_start(e_scale[r:P:QUADRANT, :].bitcast(I32), e_picked[E_STEP * r : P : QUADRANT, :].bitcast(I32))
 
-        def round_w(g, u):
-            dst = w_grouped[g][u][:].rearrange("p t m j -> p m j t")
-            src = w_raw[g][:].rearrange("p j (m t) -> p m j t", t=PACK)[:, :, :, PAIR * u : PAIR * (u + 1)]
-            if u == SCALAR_PAIR:
-                nc.scalar.copy(dst, src)
-            else:
-                nc.vector.tensor_copy(dst, src)
+        def round_w(g):
+            for u, low, high, engine in ROUNDS[g]:
+                first = W_PARTS[g][u]
+                dst = w_grouped[g][u][:].rearrange("p t m j -> p m j t")[:, low:high]
+                src = w_raw[g][:].rearrange("p j (m t) -> p m j t", t=PACK)[:, low:high, :, first : first + PAIR]
+                if engine == "scalar":
+                    nc.scalar.copy(dst, src)
+                else:
+                    nc.vector.tensor_copy(dst, src)
 
         def quantize_w(g):
-            for u in (SCALAR_PAIR, VECTOR_PAIR):
-                round_w(g, u)
-            for u in (VECTOR_PAIR, SCALAR_PAIR):
+            for u in range(len(W_PARTS[g])):
                 nc.vector.quantize_mx(
                     w_codes[g][u][:].bitcast(FP8X4), w_scale[g][u][:], w_grouped[g][u][:].rearrange("p t m j -> p (t m j)")
                 )
@@ -128,16 +135,17 @@ def tile_picked_yhawem_log_p_kernel(
         def hidden(b, g):
             events = slice(b * P, (b + 1) * P)
             moving = x_first[:, events] if g == 0 else x_second[b]
-            for t in TILE_ORDER:
-                cols = slice(t % PAIR * P, (t % PAIR + 1) * P)
+            order = [(u, i, first + i) for u, first in enumerate(W_PARTS[g]) for i in range(PAIR)]
+            for u, i, t in order:
+                cols = slice(i * P, (i + 1) * P)
                 nc.tensor.matmul_mx(
                     out=h_acc[b][:, t, :],
-                    lhsT=w_codes[g][t // PAIR][:, cols].bitcast(FP8X4),
-                    lhsT_scale=w_scale[g][t // PAIR][:, cols],
+                    lhsT=w_codes[g][u][:, cols].bitcast(FP8X4),
+                    lhsT_scale=w_scale[g][u][:, cols],
                     rhs=moving.bitcast(FP8X4),
                     rhs_scale=x_scale[PACK * g : P, events],
-                    start=g == 0 and t == TILE_ORDER[0],
-                    stop=g == PASSES - 1 and t == TILE_ORDER[-1],
+                    start=g == 0 and t == order[0][2],
+                    stop=g == PASSES - 1 and t == order[-1][2],
                 )
 
         def rectify(b):
@@ -150,21 +158,19 @@ def tile_picked_yhawem_log_p_kernel(
                 nc.scalar.activation(dst, src, ACT.Relu)
 
         def quantize_h(group):
-            bs = H_GROUPS[group]
             nc.vector.quantize_mx(
-                h_codes[:, bs[0] * P : (bs[-1] + 1) * P].bitcast(FP8X4),
-                h_scale[group][:],
-                h_grouped[group][:].rearrange("p b n t -> p (b n t)"),
+                h_codes[group][:].bitcast(FP8X4), h_scale[group][:], h_grouped[group][:].rearrange("p b n t -> p (b n t)")
             )
 
         def score(b):
             group, slot = place[b]
+            cols = slice(slot * P, (slot + 1) * P)
             nc.tensor.matmul_mx(
                 out=y_acc[b][:],
-                lhsT=h_codes[:, b * P : (b + 1) * P].bitcast(FP8X4),
-                lhsT_scale=h_scale[group][:, slot * P : (slot + 1) * P],
+                lhsT=h_codes[group][:, cols].bitcast(FP8X4),
+                lhsT_scale=h_scale[group][:, cols],
                 rhs=e_codes[:].bitcast(FP8X4),
-                rhs_scale=e_scale[E_FIRST:P, :],
+                rhs_scale=e_scale[:],
                 start=True,
                 stop=True,
             )
@@ -192,34 +198,38 @@ def tile_picked_yhawem_log_p_kernel(
         nc.gpsimd.memset(ones[:], 1.0)
         nc.scalar.activation(floor[:], ones[:], ACT.Copy, scale=0.05)
         nc.gpsimd.memset(mu_rows[:], 0.0)
+        nc.gpsimd.dma_start(e_scale_table[0:P:E_STEP, :].bitcast(I32), e_scales[0].bitcast(I32))
+        nc.gpsimd.memset(e_scale[:].bitcast(I32), 0)
 
         load_x(0)
         nc.sync.dma_start(x_list[:], offs)
         load_x_scales()
         load_w(0)
         nc.sync.dma_start(e_list[:], past)
-        load_e_scales()
+        nc.sync.dma_start(mu_rows[:BLOCKS, :], mu.rearrange("(b p) o -> b (p o)", p=P))
         load_w(1)
         load_x(1)
         nc.sync.dma_start(e_table[:].bitcast(I32), e_words[0].rearrange("p n t -> p (n t)").bitcast(I32))
-        nc.sync.dma_start(mu_rows[:BLOCKS, :], mu.rearrange("(b p) o -> b (p o)", p=P))
-        for b in AGO_ORDER:
-            nc.sync.dma_start(ago_sb[b][:], ago[b * P : (b + 1) * P, :])
-        for b in BEFORE_ORDER:
-            nc.sync.dma_start(before_sb[b][:], before[b * P : (b + 1) * P, :])
         make_identity(nc, identity[:])
         mu_turned = psum.tile([P, P], F32, name="mu_turned", tag=f"y_acc{LAST}")
         nc.tensor.transpose(mu_turned[:], mu_rows[:], identity[:])
-        nc.vector.tensor_copy(mu_sb[:], mu_turned[:, :BLOCKS])
+        nc.scalar.copy(mu_sb[:], mu_turned[:, :BLOCKS])
         y_acc = [psum.tile([P, V], F32, name=f"y_acc{b}", tag=f"y_acc{b}") for b in range(BLOCKS)]
 
         nc.vector.tensor_copy(x_scale[:], x_scale_table[:].indirect(x_list[:]))
         nc.vector.tensor_copy(x_first[:], x_table[0][:].indirect(x_list[:]))
-        nc.vector.tensor_copy(e_scale[:], e_scale_table[:].indirect(e_list[:]))
+        round_w(0)
+        nc.vector.tensor_copy(e_picked[:], e_scale_table[:].indirect(e_list[:]))
+        move_e_scales()
         quantize_w(0)
         for b in range(BLOCKS):
             hidden(b, 0)
+        round_w(1)
         quantize_w(1)
+        for b in AGO_ORDER:
+            nc.sync.dma_start(ago_sb[b][:], ago[b * P : (b + 1) * P, :])
+        for b in BEFORE_ORDER:
+            nc.sync.dma_start(before_sb[b][:], before[b * P : (b + 1) * P, :])
         for b in range(BLOCKS):
             gather_x_second(b)
             hidden(b, 1)
@@ -227,7 +237,7 @@ def tile_picked_yhawem_log_p_kernel(
                 rectify(b)
         nc.vector.tensor_copy(e_codes[:], e_table[:].indirect(e_list[:]))
         for group, bs in enumerate(H_GROUPS):
-            if bs == [LAST]:
+            if group == 1:
                 rectify(LAST)
             quantize_h(group)
             for b in bs:

@@ -1,3 +1,4 @@
+import math
 from contextlib import ExitStack
 
 import concourse.mybir as mybir
@@ -34,8 +35,9 @@ ROUNDS = [
 ]
 LAST = BLOCKS - 1
 AGO_ORDER = [0, LAST, 1, 2]
+SHARE_ORDER = [LAST, 0, 1, 2]
 BEFORE_ORDER = [LAST, 0, 1, 2]
-STORE_PARTS = [1, 1, 2, 1]
+STORE_PARTS = [1, 1, 1, 1]
 
 
 def tile_picked_yhawem_log_p_kernel(
@@ -60,7 +62,9 @@ def tile_picked_yhawem_log_p_kernel(
         raw_start = W * 4
         w_raw = [reuse.tile([P, PACK, H], F32, name=f"w_raw{g}", offset=raw_start + g * raw_bytes, align_bytes=64) for g in range(PASSES)]
         mu_sb = tile([P, BLOCKS], F32, "mu_sb")
-        ago_sb = [reuse.tile([P, V], F32, name=f"ago{b}", offset=raw_start + b * V * 4, align_bytes=64) for b in range(BLOCKS)]
+        ago_first = reuse.tile([P, PAIR, V], F32, name="ago_first", offset=raw_start, align_bytes=64)
+        ago_rest = [reuse.tile([P, V], F32, name=f"ago{b}", offset=raw_start + (b + 1) * V * 4, align_bytes=64) for b in (1, 2)]
+        ago_sb = [ago_first[:, 0, :], ago_rest[0][:], ago_rest[1][:], ago_first[:, 1, :]]
         before_sb = [
             reuse.tile([P, V], F32, name=f"before{b}", offset=raw_start + raw_bytes + b * V * 4, align_bytes=64) for b in range(BLOCKS)
         ]
@@ -86,12 +90,19 @@ def tile_picked_yhawem_log_p_kernel(
             reuse.tile([P, len(bs) * P], U32, name=f"h_codes{i}", offset=bs[0] * P * 4, align_bytes=64) for i, bs in enumerate(H_GROUPS)
         ]
         place = {b: (i, bs.index(b)) for i, bs in enumerate(H_GROUPS) for b in bs}
-        decay = [tile([P, V], F32, f"decay{b}") for b in range(BLOCKS)]
+        tail_start = raw_start + PASSES * raw_bytes
+        decay = [
+            reuse.tile([P, V], F32, name=f"decay{b}", offset=tail_start + (b - 2) * V * 4, align_bytes=64)
+            if b >= 2
+            else tile([P, V], F32, f"decay{b}")
+            for b in range(BLOCKS)
+        ]
         partial = [tile([P, V], F32, f"partial{b}") for b in range(BLOCKS)]
         mu_rows = tile([P, P], F32, "mu_rows")
         identity = tile([P, P], F32, "identity")
         ones = tile([P, 1], F32, "ones")
-        floor = tile([P, 1], F32, "floor")
+        started = tile([P, 1], F32, "started")
+        floor = reuse.tile([P, 1], F32, name="floor", offset=raw_start + 3 * V * 4, align_bytes=64)
         h_acc = [psum.tile([P, PACK, P], F32, name=f"h_acc{b}") for b in range(BLOCKS)]
 
         def load_x(g):
@@ -176,16 +187,23 @@ def tile_picked_yhawem_log_p_kernel(
             )
 
         def share(b):
-            gg = tile([P, V], F32, f"gg{b}", tag=f"decay{AGO_ORDER[-1]}" if b == 0 else None)
+            turn = SHARE_ORDER.index(b)
+            if turn == 1:
+                gg = reuse.tile([P, V], F32, name=f"gg{b}", offset=tail_start + V * 2, align_bytes=64)
+            else:
+                gg = tile([P, V], F32, f"gg{b}", tag=f"total{SHARE_ORDER[turn - 2]}" if turn else None)
             total = tile([P, 1], F32, f"total{b}")
             if b == LAST:
                 nc.vector.scalar_tensor_tensor(gg[:], y_acc[b][:], 0.0, partial[b][:], ALU.max, ALU.mult, accum_out=total[:])
             else:
                 nc.vector.scalar_tensor_tensor(gg[:], partial[b][:], 1.0, before_sb[b][:], ALU.mult, ALU.mult, accum_out=total[:])
             lam = tile([P, 1], F32, f"lam{b}")
-            nc.vector.tensor_scalar(lam[:], total[:], mu_sb[:, b : b + 1], 1.0 / 50.0, ALU.add, ALU.mult)
+            nc.scalar.activation(lam[:], total[:], ACT.Identity, bias=mu_sb[:, b : b + 1], scale=1.0 / 50.0)
             factor = tile([P, 1], F32, f"factor{b}")
             nc.vector.reciprocal(factor[:], lam[:])
+            return gg, factor
+
+        def finish(b, gg, factor):
             width = V // STORE_PARTS[b]
             for c in range(STORE_PARTS[b]):
                 cols = slice(c * width, (c + 1) * width)
@@ -196,7 +214,7 @@ def tile_picked_yhawem_log_p_kernel(
         nc.gpsimd.memset(x_scale_table[:].bitcast(I32), 0)
         nc.vector.memset(e_scale_table[:].bitcast(I32), 0)
         nc.gpsimd.memset(ones[:], 1.0)
-        nc.scalar.activation(floor[:], ones[:], ACT.Copy, scale=0.05)
+        nc.scalar.activation(started[:], ones[:], ACT.Copy, scale=math.exp(0.05))
         nc.gpsimd.memset(mu_rows[:], 0.0)
         nc.gpsimd.dma_start(e_scale_table[0:P:E_STEP, :].bitcast(I32), e_scales[0].bitcast(I32))
         nc.gpsimd.memset(e_scale[:].bitcast(I32), 0)
@@ -213,7 +231,7 @@ def tile_picked_yhawem_log_p_kernel(
         make_identity(nc, identity[:])
         mu_turned = psum.tile([P, P], F32, name="mu_turned", tag=f"y_acc{LAST}")
         nc.tensor.transpose(mu_turned[:], mu_rows[:], identity[:])
-        nc.scalar.copy(mu_sb[:], mu_turned[:, :BLOCKS])
+        nc.scalar.activation(mu_sb[:], mu_turned[:, :BLOCKS], ACT.Copy, scale=1.0 / 50.0)
         y_acc = [psum.tile([P, V], F32, name=f"y_acc{b}", tag=f"y_acc{b}") for b in range(BLOCKS)]
 
         nc.vector.tensor_copy(x_scale[:], x_scale_table[:].indirect(x_list[:]))
@@ -226,8 +244,9 @@ def tile_picked_yhawem_log_p_kernel(
             hidden(b, 0)
         round_w(1)
         quantize_w(1)
-        for b in AGO_ORDER:
-            nc.sync.dma_start(ago_sb[b][:], ago[b * P : (b + 1) * P, :])
+        nc.sync.dma_start(ago_first[:], ago.rearrange("(b p) v -> p b v", p=P)[:, 0:BLOCKS:LAST, :])
+        for b in AGO_ORDER[PAIR:]:
+            nc.sync.dma_start(ago_sb[b], ago[b * P : (b + 1) * P, :])
         for b in BEFORE_ORDER:
             nc.sync.dma_start(before_sb[b][:], before[b * P : (b + 1) * P, :])
         for b in range(BLOCKS):
@@ -243,9 +262,11 @@ def tile_picked_yhawem_log_p_kernel(
             for b in bs:
                 score(b)
         for b in AGO_ORDER:
-            nc.scalar.activation(decay[b][:], ago_sb[b][:], ACT.Exp, scale=-0.7)
+            nc.scalar.activation(decay[b][:], ago_sb[b], ACT.Exp, scale=-0.7)
         nc.gpsimd.tensor_tensor(partial[LAST][:], decay[LAST][:], before_sb[LAST][:], ALU.mult)
         for b in range(LAST):
             nc.vector.scalar_tensor_tensor(partial[b][:], y_acc[b][:], 0.0, decay[b][:], ALU.max, ALU.mult)
-        for b in AGO_ORDER:
-            share(b)
+        nc.scalar.activation(floor[:], started[:], ACT.Ln)
+        shares = [share(b) for b in SHARE_ORDER]
+        for b, (gg, factor) in zip(SHARE_ORDER, shares):
+            finish(b, gg, factor)

@@ -27,16 +27,16 @@ LIST_ROWS = 16
 PAIR = 2
 SCALAR_PAIR, VECTOR_PAIR = 0, 1
 E_STEP = 8
-H_GROUPS = [[0, 1], [2], [3]]
+H_GROUPS = [[2], [0, 1], [3]]
 W_PARTS = [[0, 2], [2, 0]]
 ROUNDS = [
     [(1, 0, P // 2, "vector"), (0, 0, P, "scalar"), (1, P // 2, P, "scalar")],
     [(0, 0, P, "vector"), (1, 0, P, "scalar")],
 ]
 LAST = BLOCKS - 1
-AGO_ORDER = [0, LAST, 1, 2]
-SHARE_ORDER = [LAST, 0, 1, 2]
-BEFORE_ORDER = [LAST, 0, 1, 2]
+AGO_ORDER = [2, LAST, 0, 1]
+SHARE_ORDER = [LAST, 2, 0, 1]
+BEFORE_ORDER = SHARE_ORDER
 STORE_PARTS = [1, 1, 1, 1]
 
 
@@ -63,8 +63,8 @@ def tile_picked_yhawem_log_p_kernel(
         w_raw = [reuse.tile([P, PACK, H], F32, name=f"w_raw{g}", offset=raw_start + g * raw_bytes, align_bytes=64) for g in range(PASSES)]
         mu_sb = tile([P, BLOCKS], F32, "mu_sb")
         ago_first = reuse.tile([P, PAIR, V], F32, name="ago_first", offset=raw_start, align_bytes=64)
-        ago_rest = [reuse.tile([P, V], F32, name=f"ago{b}", offset=raw_start + (b + 1) * V * 4, align_bytes=64) for b in (1, 2)]
-        ago_sb = [ago_first[:, 0, :], ago_rest[0][:], ago_rest[1][:], ago_first[:, 1, :]]
+        ago_rest = [reuse.tile([P, V], F32, name=f"ago{b}", offset=raw_start + (b + PAIR) * V * 4, align_bytes=64) for b in (0, 1)]
+        ago_sb = [ago_rest[0][:], ago_rest[1][:], ago_first[:, 0, :], ago_first[:, 1, :]]
         before_sb = [
             reuse.tile([P, V], F32, name=f"before{b}", offset=raw_start + raw_bytes + b * V * 4, align_bytes=64) for b in range(BLOCKS)
         ]
@@ -73,7 +73,9 @@ def tile_picked_yhawem_log_p_kernel(
         e_codes = tile([P, V], U32, "e_codes")
         w_grouped = [[tile([P, PAIR, P, PACK], BF16, f"w_grouped{g}_{u}") for u in range(PACK // PAIR)] for g in range(PASSES)]
         x_head = tile([P, P], U32, "x_head")
-        x_rest = tile([P, BLOCKS - 1, P], U32, "x_rest", tag="w_grouped1_1")
+        x_rest = reuse.tile(
+            [P, BLOCKS - 1, P], U32, name="x_rest", offset=raw_start + raw_bytes + BEFORE_ORDER[-1] * V * 4, align_bytes=64
+        )
         x_second = [x_head[:]] + [x_rest[:, b, :] for b in range(BLOCKS - 1)]
         e_picked = tile([P, V], U8, "e_picked")
         e_scale = tile([P, V], U8, "e_scale")
@@ -87,17 +89,22 @@ def tile_picked_yhawem_log_p_kernel(
         ]
         h_scale = [tile([P, len(bs) * P], U8, f"h_scale{i}") for i, bs in enumerate(H_GROUPS)]
         h_codes = [
-            reuse.tile([P, len(bs) * P], U32, name=f"h_codes{i}", offset=bs[0] * P * 4, align_bytes=64) for i, bs in enumerate(H_GROUPS)
+            reuse.tile([P, len(bs) * P], U32, name=f"h_codes{i}", offset=bs[0] * P * 4, align_bytes=64)
+            if i
+            else tile([P, P], U32, "h_codes0")
+            for i, bs in enumerate(H_GROUPS)
         ]
         place = {b: (i, bs.index(b)) for i, bs in enumerate(H_GROUPS) for b in bs}
         tail_start = raw_start + PASSES * raw_bytes
+        held = {AGO_ORDER[-1]: 0, LAST: 1}
         decay = [
-            reuse.tile([P, V], F32, name=f"decay{b}", offset=tail_start + (b - 2) * V * 4, align_bytes=64)
-            if b >= 2
+            reuse.tile([P, V], F32, name=f"decay{b}", offset=tail_start + held[b] * V * 4, align_bytes=64)
+            if b in held
             else tile([P, V], F32, f"decay{b}")
             for b in range(BLOCKS)
         ]
-        partial = [tile([P, V], F32, f"partial{b}") for b in range(BLOCKS)]
+        partial = [tile([P, V], F32, f"partial{b}") for b in range(LAST)]
+        partial.append(reuse.tile([P, V], F32, name="mask", offset=S * 4, align_bytes=64))
         mu_rows = tile([P, P], F32, "mu_rows")
         identity = tile([P, P], F32, "identity")
         ones = tile([P, 1], F32, "ones")
@@ -244,16 +251,18 @@ def tile_picked_yhawem_log_p_kernel(
             hidden(b, 0)
         round_w(1)
         quantize_w(1)
-        nc.sync.dma_start(ago_first[:], ago.rearrange("(b p) v -> p b v", p=P)[:, 0:BLOCKS:LAST, :])
+        nc.sync.dma_start(ago_first[:], ago.rearrange("(b p) v -> p b v", p=P)[:, PAIR:, :])
         for b in AGO_ORDER[PAIR:]:
             nc.sync.dma_start(ago_sb[b], ago[b * P : (b + 1) * P, :])
-        for b in BEFORE_ORDER:
+        for b in BEFORE_ORDER[:-1]:
             nc.sync.dma_start(before_sb[b][:], before[b * P : (b + 1) * P, :])
         for b in range(BLOCKS):
             gather_x_second(b)
             hidden(b, 1)
             if b != LAST:
                 rectify(b)
+        for b in BEFORE_ORDER[-1:]:
+            nc.sync.dma_start(before_sb[b][:], before[b * P : (b + 1) * P, :])
         nc.vector.tensor_copy(e_codes[:], e_table[:].indirect(e_list[:]))
         for group, bs in enumerate(H_GROUPS):
             if group == 1:
@@ -264,7 +273,7 @@ def tile_picked_yhawem_log_p_kernel(
         for b in AGO_ORDER:
             nc.scalar.activation(decay[b][:], ago_sb[b], ACT.Exp, scale=-0.7)
         nc.gpsimd.tensor_tensor(partial[LAST][:], decay[LAST][:], before_sb[LAST][:], ALU.mult)
-        for b in range(LAST):
+        for b in SHARE_ORDER[1:]:
             nc.vector.scalar_tensor_tensor(partial[b][:], y_acc[b][:], 0.0, decay[b][:], ALU.max, ALU.mult)
         nc.scalar.activation(floor[:], started[:], ACT.Ln)
         shares = [share(b) for b in SHARE_ORDER]

@@ -20,24 +20,26 @@ ACT = mybir.ActivationFunctionType
 P = 128
 PACK = 4
 QUADRANT = 32
+WORD = 4
 K_PASS = P * PACK
 PASSES = K // K_PASS
 BLOCKS = S // P
 LIST_ROWS = 16
+ROW = V * WORD
+RATE, GAIN, FLOOR = 0.7, 50.0, 0.05
+
+E_STEP = QUADRANT // PACK
 PAIR = 2
-SCALAR_PAIR, VECTOR_PAIR = 0, 1
-E_STEP = 8
-H_GROUPS = [[2], [0, 1], [3]]
-W_PARTS = [[0, 2], [2, 0]]
+PAIR_FIRST = [[0, 2], [2, 0]]
 ROUNDS = [
     [(1, 0, P // 2, "vector"), (0, 0, P, "scalar"), (1, P // 2, P, "scalar")],
     [(0, 0, P, "vector"), (1, 0, P, "scalar")],
 ]
 LAST = BLOCKS - 1
-AGO_ORDER = [2, LAST, 0, 1]
-SHARE_ORDER = [LAST, 2, 0, 1]
-BEFORE_ORDER = SHARE_ORDER
-STORE_PARTS = [1, 1, 1, 1]
+H_GROUPS = [[2], [0, 1], [LAST]]
+DECAY_ORDER = [2, LAST, 0, 1]
+SUM_ORDER = [LAST, 2, 0, 1]
+LAST_PARTS = 2
 
 
 def tile_picked_yhawem_log_p_kernel(
@@ -52,72 +54,70 @@ def tile_picked_yhawem_log_p_kernel(
         def tile(shape, dtype, name, tag=None):
             return keep.tile(shape, dtype, name=name, tag=tag or name, align_bytes=64)
 
+        def placed(shape, dtype, name, offset):
+            return reuse.tile(shape, dtype, name=name, offset=offset, align_bytes=64)
+
+        raw_at = [W * WORD + g * PACK * H * WORD for g in range(PASSES)]
+        decay_at = raw_at[-1] + PACK * H * WORD
+
         x_list = tile([P, S // LIST_ROWS], U16, "x_list")
         e_list = tile([P, V // LIST_ROWS], U16, "e_list")
         x_scale_table = tile([P, T], U8, "x_scale_table")
         e_scale_table = tile([P, W], U8, "e_scale_table")
         x_table = [tile([P, T], U32, f"x_table{g}") for g in range(PASSES)]
-        e_table = reuse.tile([P, W], U32, name="e_table", offset=0, align_bytes=64)
-        raw_bytes = PACK * H * 4
-        raw_start = W * 4
-        w_raw = [reuse.tile([P, PACK, H], F32, name=f"w_raw{g}", offset=raw_start + g * raw_bytes, align_bytes=64) for g in range(PASSES)]
-        mu_sb = tile([P, BLOCKS], F32, "mu_sb")
-        ago_first = reuse.tile([P, PAIR, V], F32, name="ago_first", offset=raw_start, align_bytes=64)
-        ago_rest = [reuse.tile([P, V], F32, name=f"ago{b}", offset=raw_start + (b + PAIR) * V * 4, align_bytes=64) for b in (0, 1)]
-        ago_sb = [ago_rest[0][:], ago_rest[1][:], ago_first[:, 0, :], ago_first[:, 1, :]]
-        before_sb = [
-            reuse.tile([P, V], F32, name=f"before{b}", offset=raw_start + raw_bytes + b * V * 4, align_bytes=64) for b in range(BLOCKS)
-        ]
+        e_table = placed([P, W], U32, "e_table", 0)
+        w_raw = [placed([P, PACK, H], F32, f"w_raw{g}", raw_at[g]) for g in range(PASSES)]
+        mu_part = tile([P, BLOCKS], F32, "mu_part")
+        ago_upper = placed([P, PAIR, V], F32, "ago_upper", raw_at[0])
+        ago_sb = [placed([P, V], F32, f"ago{b}", raw_at[0] + (PAIR + b) * ROW)[:] for b in range(PAIR)]
+        ago_sb += [ago_upper[:, b, :] for b in range(PAIR)]
+        before_sb = [placed([P, V], F32, f"before{b}", raw_at[1] + b * ROW) for b in range(BLOCKS)]
         x_scale = tile([P, S], U8, "x_scale")
         x_first = tile([P, S], U32, "x_first")
         e_codes = tile([P, V], U32, "e_codes")
         w_grouped = [[tile([P, PAIR, P, PACK], BF16, f"w_grouped{g}_{u}") for u in range(PACK // PAIR)] for g in range(PASSES)]
         x_head = tile([P, P], U32, "x_head")
-        x_rest = reuse.tile(
-            [P, BLOCKS - 1, P], U32, name="x_rest", offset=raw_start + raw_bytes + BEFORE_ORDER[-1] * V * 4, align_bytes=64
-        )
+        x_rest = placed([P, BLOCKS - 1, P], U32, "x_rest", raw_at[1] + SUM_ORDER[-1] * ROW)
         x_second = [x_head[:]] + [x_rest[:, b, :] for b in range(BLOCKS - 1)]
         e_picked = tile([P, V], U8, "e_picked")
         e_scale = tile([P, V], U8, "e_scale")
         w_codes = [[tile([P, PAIR * P], U32, f"w_codes{g}_{u}") for u in range(PACK // PAIR)] for g in range(PASSES)]
         w_scale = [[tile([P, PAIR * P], U8, f"w_scale{g}_{u}") for u in range(PACK // PAIR)] for g in range(PASSES)]
+        rectified_at = S * WORD
         h_grouped = [
-            reuse.tile([P, len(bs), P, PACK], BF16, name=f"h_grouped{i}", offset=S * 4, align_bytes=64)
+            placed([P, len(bs), P, PACK], BF16, f"h_grouped{i}", rectified_at)
             if bs == [LAST]
             else tile([P, len(bs), P, PACK], BF16, f"h_grouped{i}")
             for i, bs in enumerate(H_GROUPS)
         ]
         h_scale = [tile([P, len(bs) * P], U8, f"h_scale{i}") for i, bs in enumerate(H_GROUPS)]
         h_codes = [
-            reuse.tile([P, len(bs) * P], U32, name=f"h_codes{i}", offset=bs[0] * P * 4, align_bytes=64)
-            if i
-            else tile([P, P], U32, "h_codes0")
+            placed([P, len(bs) * P], U32, f"h_codes{i}", bs[0] * P * WORD) if i else tile([P, len(bs) * P], U32, f"h_codes{i}")
             for i, bs in enumerate(H_GROUPS)
         ]
         place = {b: (i, bs.index(b)) for i, bs in enumerate(H_GROUPS) for b in bs}
-        tail_start = raw_start + PASSES * raw_bytes
-        held = {AGO_ORDER[-1]: 0, LAST: 1}
+        decay_slot = {DECAY_ORDER[-1]: 0, LAST: 1}
         decay = [
-            reuse.tile([P, V], F32, name=f"decay{b}", offset=tail_start + held[b] * V * 4, align_bytes=64)
-            if b in held
-            else tile([P, V], F32, f"decay{b}")
+            placed([P, V], F32, f"decay{b}", decay_at + decay_slot[b] * ROW) if b in decay_slot else tile([P, V], F32, f"decay{b}")
             for b in range(BLOCKS)
         ]
         partial = [tile([P, V], F32, f"partial{b}") for b in range(LAST)]
-        partial.append(reuse.tile([P, V], F32, name="mask", offset=S * 4, align_bytes=64))
+        partial.append(placed([P, V], F32, f"partial{LAST}", rectified_at))
         mu_rows = tile([P, P], F32, "mu_rows")
         identity = tile([P, P], F32, "identity")
         ones = tile([P, 1], F32, "ones")
-        started = tile([P, 1], F32, "started")
-        floor = reuse.tile([P, 1], F32, name="floor", offset=raw_start + 3 * V * 4, align_bytes=64)
+        exp_floor = tile([P, 1], F32, "exp_floor")
+        floor = placed([P, 1], F32, "floor", raw_at[0] + (PAIR + DECAY_ORDER[-1]) * ROW)
         h_acc = [psum.tile([P, PACK, P], F32, name=f"h_acc{b}") for b in range(BLOCKS)]
+
+        def rows(b):
+            return slice(b * P, (b + 1) * P)
 
         def load_x(g):
             nc.sync.dma_start(x_table[g][:].bitcast(I32), x_words[g].rearrange("p n t -> p (n t)").bitcast(I32))
 
         def load_w(g):
-            rows = slice(g * K_PASS, (g + 1) * K_PASS)
-            nc.sync.dma_start(w_raw[g][:], w1[rows, :].rearrange("(p j) c -> p j c", j=PACK))
+            nc.sync.dma_start(w_raw[g][:], w1[g * K_PASS : (g + 1) * K_PASS, :].rearrange("(p j) c -> p j c", j=PACK))
 
         def load_x_scales():
             for q in range(P // QUADRANT):
@@ -132,7 +132,7 @@ def tile_picked_yhawem_log_p_kernel(
 
         def round_w(g):
             for u, low, high, engine in ROUNDS[g]:
-                first = W_PARTS[g][u]
+                first = PAIR_FIRST[g][u]
                 dst = w_grouped[g][u][:].rearrange("p t m j -> p m j t")[:, low:high]
                 src = w_raw[g][:].rearrange("p j (m t) -> p m j t", t=PACK)[:, low:high, :, first : first + PAIR]
                 if engine == "scalar":
@@ -141,7 +141,7 @@ def tile_picked_yhawem_log_p_kernel(
                     nc.vector.tensor_copy(dst, src)
 
         def quantize_w(g):
-            for u in range(len(W_PARTS[g])):
+            for u in range(PACK // PAIR):
                 nc.vector.quantize_mx(
                     w_codes[g][u][:].bitcast(FP8X4), w_scale[g][u][:], w_grouped[g][u][:].rearrange("p t m j -> p (t m j)")
                 )
@@ -151,19 +151,17 @@ def tile_picked_yhawem_log_p_kernel(
             nc.vector.tensor_copy(x_second[b], x_table[1][:].indirect(entries))
 
         def hidden(b, g):
-            events = slice(b * P, (b + 1) * P)
-            moving = x_first[:, events] if g == 0 else x_second[b]
-            order = [(u, i, first + i) for u, first in enumerate(W_PARTS[g]) for i in range(PAIR)]
-            for u, i, t in order:
-                cols = slice(i * P, (i + 1) * P)
+            moving = x_first[:, rows(b)] if g == 0 else x_second[b]
+            for n in range(PACK):
+                u, i = divmod(n, PAIR)
                 nc.tensor.matmul_mx(
-                    out=h_acc[b][:, t, :],
-                    lhsT=w_codes[g][u][:, cols].bitcast(FP8X4),
-                    lhsT_scale=w_scale[g][u][:, cols],
+                    out=h_acc[b][:, PAIR_FIRST[g][u] + i, :],
+                    lhsT=w_codes[g][u][:, rows(i)].bitcast(FP8X4),
+                    lhsT_scale=w_scale[g][u][:, rows(i)],
                     rhs=moving.bitcast(FP8X4),
-                    rhs_scale=x_scale[PACK * g : P, events],
-                    start=g == 0 and t == order[0][2],
-                    stop=g == PASSES - 1 and t == order[-1][2],
+                    rhs_scale=x_scale[PACK * g : P, rows(b)],
+                    start=g == 0 and n == 0,
+                    stop=g == PASSES - 1 and n == PACK - 1,
                 )
 
         def rectify(b):
@@ -182,46 +180,48 @@ def tile_picked_yhawem_log_p_kernel(
 
         def score(b):
             group, slot = place[b]
-            cols = slice(slot * P, (slot + 1) * P)
             nc.tensor.matmul_mx(
                 out=y_acc[b][:],
-                lhsT=h_codes[group][:, cols].bitcast(FP8X4),
-                lhsT_scale=h_scale[group][:, cols],
+                lhsT=h_codes[group][:, rows(slot)].bitcast(FP8X4),
+                lhsT_scale=h_scale[group][:, rows(slot)],
                 rhs=e_codes[:].bitcast(FP8X4),
                 rhs_scale=e_scale[:],
                 start=True,
                 stop=True,
             )
 
-        def share(b):
-            turn = SHARE_ORDER.index(b)
+        def share(turn, b):
             if turn == 1:
-                gg = reuse.tile([P, V], F32, name=f"gg{b}", offset=tail_start + V * 2, align_bytes=64)
+                gg = placed([P, V], F32, f"gg{b}", decay_at + ROW // 2)
             else:
-                gg = tile([P, V], F32, f"gg{b}", tag=f"total{SHARE_ORDER[turn - 2]}" if turn else None)
+                gg = tile([P, V], F32, f"gg{b}", tag=f"total{SUM_ORDER[turn - 2]}" if turn else None)
             total = tile([P, 1], F32, f"total{b}")
             if b == LAST:
                 nc.vector.scalar_tensor_tensor(gg[:], y_acc[b][:], 0.0, partial[b][:], ALU.max, ALU.mult, accum_out=total[:])
             else:
                 nc.vector.scalar_tensor_tensor(gg[:], partial[b][:], 1.0, before_sb[b][:], ALU.mult, ALU.mult, accum_out=total[:])
-            lam = tile([P, 1], F32, f"lam{b}")
-            nc.scalar.activation(lam[:], total[:], ACT.Identity, bias=mu_sb[:, b : b + 1], scale=1.0 / 50.0)
+            lam_part = tile([P, 1], F32, f"lam_part{b}")
+            if turn == BLOCKS - 1:
+                nc.vector.tensor_scalar(lam_part[:], total[:], 1.0 / GAIN, mu_part[:, b : b + 1], ALU.mult, ALU.add)
+            else:
+                nc.scalar.activation(lam_part[:], total[:], ACT.Identity, bias=mu_part[:, b : b + 1], scale=1.0 / GAIN)
             factor = tile([P, 1], F32, f"factor{b}")
-            nc.vector.reciprocal(factor[:], lam[:])
+            nc.vector.reciprocal(factor[:], lam_part[:])
             return gg, factor
 
         def finish(b, gg, factor):
-            width = V // STORE_PARTS[b]
-            for c in range(STORE_PARTS[b]):
+            parts = LAST_PARTS if b == SUM_ORDER[-1] else 1
+            width = V // parts
+            for c in range(parts):
                 cols = slice(c * width, (c + 1) * width)
                 result = tile([P, width], F32, f"result{b}_{c}")
                 nc.scalar.activation(result[:], gg[:, cols], ACT.Ln, bias=floor[:], scale=factor[:])
-                nc.sync.dma_start(out[b * P : (b + 1) * P, cols], result[:])
+                nc.sync.dma_start(out[rows(b), cols], result[:])
 
         nc.gpsimd.memset(x_scale_table[:].bitcast(I32), 0)
         nc.vector.memset(e_scale_table[:].bitcast(I32), 0)
         nc.gpsimd.memset(ones[:], 1.0)
-        nc.scalar.activation(started[:], ones[:], ACT.Copy, scale=math.exp(0.05))
+        nc.scalar.activation(exp_floor[:], ones[:], ACT.Copy, scale=math.exp(FLOOR))
         nc.gpsimd.memset(mu_rows[:], 0.0)
         nc.gpsimd.dma_start(e_scale_table[0:P:E_STEP, :].bitcast(I32), e_scales[0].bitcast(I32))
         nc.gpsimd.memset(e_scale[:].bitcast(I32), 0)
@@ -238,7 +238,7 @@ def tile_picked_yhawem_log_p_kernel(
         make_identity(nc, identity[:])
         mu_turned = psum.tile([P, P], F32, name="mu_turned", tag=f"y_acc{LAST}")
         nc.tensor.transpose(mu_turned[:], mu_rows[:], identity[:])
-        nc.scalar.activation(mu_sb[:], mu_turned[:, :BLOCKS], ACT.Copy, scale=1.0 / 50.0)
+        nc.scalar.activation(mu_part[:], mu_turned[:, :BLOCKS], ACT.Copy, scale=1.0 / GAIN)
         y_acc = [psum.tile([P, V], F32, name=f"y_acc{b}", tag=f"y_acc{b}") for b in range(BLOCKS)]
 
         nc.vector.tensor_copy(x_scale[:], x_scale_table[:].indirect(x_list[:]))
@@ -251,18 +251,17 @@ def tile_picked_yhawem_log_p_kernel(
             hidden(b, 0)
         round_w(1)
         quantize_w(1)
-        nc.sync.dma_start(ago_first[:], ago.rearrange("(b p) v -> p b v", p=P)[:, PAIR:, :])
-        for b in AGO_ORDER[PAIR:]:
-            nc.sync.dma_start(ago_sb[b], ago[b * P : (b + 1) * P, :])
-        for b in BEFORE_ORDER[:-1]:
-            nc.sync.dma_start(before_sb[b][:], before[b * P : (b + 1) * P, :])
+        nc.sync.dma_start(ago_upper[:], ago.rearrange("(b p) v -> p b v", p=P)[:, PAIR:, :])
+        for b in DECAY_ORDER[PAIR:]:
+            nc.sync.dma_start(ago_sb[b], ago[rows(b), :])
+        for b in SUM_ORDER[:-1]:
+            nc.sync.dma_start(before_sb[b][:], before[rows(b), :])
         for b in range(BLOCKS):
             gather_x_second(b)
             hidden(b, 1)
             if b != LAST:
                 rectify(b)
-        for b in BEFORE_ORDER[-1:]:
-            nc.sync.dma_start(before_sb[b][:], before[b * P : (b + 1) * P, :])
+        nc.sync.dma_start(before_sb[SUM_ORDER[-1]][:], before[rows(SUM_ORDER[-1]), :])
         nc.vector.tensor_copy(e_codes[:], e_table[:].indirect(e_list[:]))
         for group, bs in enumerate(H_GROUPS):
             if group == 1:
@@ -270,12 +269,12 @@ def tile_picked_yhawem_log_p_kernel(
             quantize_h(group)
             for b in bs:
                 score(b)
-        for b in AGO_ORDER:
-            nc.scalar.activation(decay[b][:], ago_sb[b], ACT.Exp, scale=-0.7)
+        for b in DECAY_ORDER:
+            nc.scalar.activation(decay[b][:], ago_sb[b], ACT.Exp, scale=-RATE)
         nc.gpsimd.tensor_tensor(partial[LAST][:], decay[LAST][:], before_sb[LAST][:], ALU.mult)
-        for b in SHARE_ORDER[1:]:
+        for b in SUM_ORDER[1:]:
             nc.vector.scalar_tensor_tensor(partial[b][:], y_acc[b][:], 0.0, decay[b][:], ALU.max, ALU.mult)
-        nc.scalar.activation(floor[:], started[:], ACT.Ln)
-        shares = [share(b) for b in SHARE_ORDER]
-        for b, (gg, factor) in zip(SHARE_ORDER, shares):
+        nc.scalar.activation(floor[:], exp_floor[:], ACT.Ln)
+        shares = [share(turn, b) for turn, b in enumerate(SUM_ORDER)]
+        for b, (gg, factor) in zip(SUM_ORDER, shares):
             finish(b, gg, factor)

@@ -201,10 +201,7 @@ def tile_picked_yhawem_log_p_kernel(
             else:
                 nc.vector.scalar_tensor_tensor(gg[:], partial[b][:], 1.0, before_sb[b][:], ALU.mult, ALU.mult, accum_out=total[:])
             lam_part = tile([P, 1], F32, f"lam_part{b}")
-            if turn == BLOCKS - 1:
-                nc.vector.tensor_scalar(lam_part[:], total[:], 1.0 / GAIN, mu_part[:, b : b + 1], ALU.mult, ALU.add)
-            else:
-                nc.scalar.activation(lam_part[:], total[:], ACT.Identity, bias=mu_part[:, b : b + 1], scale=1.0 / GAIN)
+            nc.scalar.activation(lam_part[:], total[:], ACT.Identity, bias=mu_part[:, b : b + 1], scale=1.0 / GAIN)
             factor = tile([P, 1], F32, f"factor{b}")
             nc.vector.reciprocal(factor[:], lam_part[:])
             return gg, factor

@@ -52,10 +52,10 @@ def tile_picked_yhawem_log_p_kernel(
         psum = ctx.enter_context(tc.psum_pool(name="psum", bufs=1))
 
         def tile(shape, dtype, name, tag=None):
-            return keep.tile(shape, dtype, name=name, tag=tag or name, align_bytes=64)
+            return keep.tile(shape, dtype, name=name, tag=tag or name, align_bytes=256)
 
         def placed(shape, dtype, name, offset):
-            return reuse.tile(shape, dtype, name=name, offset=offset, align_bytes=64)
+            return reuse.tile(shape, dtype, name=name, offset=offset, align_bytes=256)
 
         raw_at = [W * WORD + g * PACK * H * WORD for g in range(PASSES)]
         decay_at = raw_at[-1] + PACK * H * WORD

@@ -166,8 +166,8 @@ def tile_picked_yhawem_log_p_kernel(
 
         def rectify(b):
             group, slot = place[b]
-            dst = h_grouped[group][:, slot]
-            src = h_acc[b][:].rearrange("p t n -> p n t")
+            dst = h_grouped[group][:, slot].rearrange("p (c i) t -> p c t i", i=PAIR)
+            src = h_acc[b][:].rearrange("p t (c i) -> p c t i", i=PAIR)
             if b == LAST:
                 nc.vector.tensor_scalar_max(dst, src, 0.0)
             else:

import math
from contextlib import ExitStack

import concourse.mybir as mybir
from concourse.masks import make_identity

K, T, S, H, V, W = 1024, 1024, 512, 512, 512, 2048
FLOPS = 2 * K * H * S + 2 * H * S * V

F32 = mybir.dt.float32
BF16 = mybir.dt.bfloat16
I32 = mybir.dt.int32
U32 = mybir.dt.uint32
U16 = mybir.dt.uint16
U8 = mybir.dt.uint8
FP8X4 = mybir.dt.float8_e4m3fn_x4
ALU = mybir.AluOpType
ACT = mybir.ActivationFunctionType

P = 128
PACK = 4
QUADRANT = 32
WORD = 4
K_PASS = P * PACK
PASSES = K // K_PASS
BLOCKS = S // P
LIST_ROWS = 16
ROW = V * WORD
RATE, GAIN, FLOOR = 0.7, 50.0, 0.05

E_STEP = QUADRANT // PACK
PAIR = 2
PAIR_FIRST = [[0, 2], [2, 0]]
ROUNDS = [
    [(1, 0, P // 2, "vector"), (0, 0, P, "scalar"), (1, P // 2, P, "scalar")],
    [(0, 0, P, "vector"), (1, 0, P, "scalar")],
]
LAST = BLOCKS - 1
H_GROUPS = [[2], [0, 1], [LAST]]
DECAY_ORDER = [2, LAST, 0, 1]
SUM_ORDER = [LAST, 2, 0, 1]
LAST_PARTS = 2


def tile_picked_yhawem_log_p_kernel(
    tc, x_words, x_scales, w1, e_words, e_scales, ago, before, mu, offs, past, out
):
    nc = tc.nc
    with ExitStack() as ctx:
        keep = ctx.enter_context(tc.tile_pool(name="keep", bufs=1))
        reuse = ctx.enter_context(tc.tile_pool(name="reuse", bufs=1))
        psum = ctx.enter_context(tc.psum_pool(name="psum", bufs=1))

        def tile(shape, dtype, name, tag=None):
            return keep.tile(shape, dtype, name=name, tag=tag or name, align_bytes=256)

        def placed(shape, dtype, name, offset):
            return reuse.tile(shape, dtype, name=name, offset=offset, align_bytes=256)

        raw_at = [W * WORD + g * PACK * H * WORD for g in range(PASSES)]
        decay_at = raw_at[-1] + PACK * H * WORD

        x_list = tile([P, S // LIST_ROWS], U16, "x_list")
        e_list = tile([P, V // LIST_ROWS], U16, "e_list")
        x_scale_table = tile([P, T], U8, "x_scale_table")
        e_scale_table = tile([P, W], U8, "e_scale_table")
        x_table = [tile([P, T], U32, f"x_table{g}") for g in range(PASSES)]
        e_table = placed([P, W], U32, "e_table", 0)
        w_raw = [placed([P, PACK, H], F32, f"w_raw{g}", raw_at[g]) for g in range(PASSES)]
        mu_part = tile([P, BLOCKS], F32, "mu_part")
        ago_upper = placed([P, PAIR, V], F32, "ago_upper", raw_at[0])
        ago_sb = [placed([P, V], F32, f"ago{b}", raw_at[0] + (PAIR + b) * ROW)[:] for b in range(PAIR)]
        ago_sb += [ago_upper[:, b, :] for b in range(PAIR)]
        before_sb = [placed([P, V], F32, f"before{b}", raw_at[1] + b * ROW) for b in range(BLOCKS)]
        x_scale = tile([P, S], U8, "x_scale")
        x_first = tile([P, S], U32, "x_first")
        e_codes = tile([P, V], U32, "e_codes")
        w_grouped = [[tile([P, PAIR, P, PACK], BF16, f"w_grouped{g}_{u}") for u in range(PACK // PAIR)] for g in range(PASSES)]
        x_head = tile([P, P], U32, "x_head")
        x_rest = placed([P, BLOCKS - 1, P], U32, "x_rest", raw_at[1] + SUM_ORDER[-1] * ROW)
        x_second = [x_head[:]] + [x_rest[:, b, :] for b in range(BLOCKS - 1)]
        e_picked = tile([P, V], U8, "e_picked")
        e_scale = tile([P, V], U8, "e_scale")
        w_codes = [[tile([P, PAIR * P], U32, f"w_codes{g}_{u}") for u in range(PACK // PAIR)] for g in range(PASSES)]
        w_scale = [[tile([P, PAIR * P], U8, f"w_scale{g}_{u}") for u in range(PACK // PAIR)] for g in range(PASSES)]
        rectified_at = S * WORD
        h_grouped = [
            placed([P, len(bs), P, PACK], BF16, f"h_grouped{i}", rectified_at)
            if bs == [LAST]
            else tile([P, len(bs), P, PACK], BF16, f"h_grouped{i}")
            for i, bs in enumerate(H_GROUPS)
        ]
        h_scale = [tile([P, len(bs) * P], U8, f"h_scale{i}") for i, bs in enumerate(H_GROUPS)]
        h_codes = [
            placed([P, len(bs) * P], U32, f"h_codes{i}", bs[0] * P * WORD) if i else tile([P, len(bs) * P], U32, f"h_codes{i}")
            for i, bs in enumerate(H_GROUPS)
        ]
        place = {b: (i, bs.index(b)) for i, bs in enumerate(H_GROUPS) for b in bs}
        decay_slot = {DECAY_ORDER[-1]: 0, LAST: 1}
        decay = [
            placed([P, V], F32, f"decay{b}", decay_at + decay_slot[b] * ROW) if b in decay_slot else tile([P, V], F32, f"decay{b}")
            for b in range(BLOCKS)
        ]
        partial = [tile([P, V], F32, f"partial{b}") for b in range(LAST)]
        partial.append(placed([P, V], F32, f"partial{LAST}", rectified_at))
        mu_rows = tile([P, P], F32, "mu_rows")
        identity = tile([P, P], F32, "identity")
        ones = tile([P, 1], F32, "ones")
        exp_floor = tile([P, 1], F32, "exp_floor")
        floor = placed([P, 1], F32, "floor", raw_at[0] + (PAIR + DECAY_ORDER[-1]) * ROW)
        h_acc = [psum.tile([P, PACK, P], F32, name=f"h_acc{b}") for b in range(BLOCKS)]

        def rows(b):
            return slice(b * P, (b + 1) * P)

        def load_x(g):
            nc.sync.dma_start(x_table[g][:].bitcast(I32), x_words[g].rearrange("p n t -> p (n t)").bitcast(I32))

        def load_w(g):
            nc.sync.dma_start(w_raw[g][:], w1[g * K_PASS : (g + 1) * K_PASS, :].rearrange("(p j) c -> p j c", j=PACK))

        def load_x_scales():
            for q in range(P // QUADRANT):
                nc.sync.dma_start(
                    x_scale_table[QUADRANT * q : QUADRANT * q + PACK * PASSES, :].bitcast(I32),
                    x_scales[:, PACK * q : PACK * (q + 1), :].bitcast(I32),
                )

        def move_e_scales():
            for r in range(PACK):
                nc.sync.dma_start(e_scale[r:P:QUADRANT, :].bitcast(I32), e_picked[E_STEP * r : P : QUADRANT, :].bitcast(I32))

        def round_w(g):
            for u, low, high, engine in ROUNDS[g]:
                first = PAIR_FIRST[g][u]
                dst = w_grouped[g][u][:].rearrange("p t m j -> p m j t")[:, low:high]
                src = w_raw[g][:].rearrange("p j (m t) -> p m j t", t=PACK)[:, low:high, :, first : first + PAIR]
                if engine == "scalar":
                    nc.scalar.copy(dst, src)
                else:
                    nc.vector.tensor_copy(dst, src)

        def quantize_w(g):
            for u in range(PACK // PAIR):
                nc.vector.quantize_mx(
                    w_codes[g][u][:].bitcast(FP8X4), w_scale[g][u][:], w_grouped[g][u][:].rearrange("p t m j -> p (t m j)")
                )

        def gather_x_second(b):
            entries = x_list[:, b * P // LIST_ROWS : (b + 1) * P // LIST_ROWS]
            nc.vector.tensor_copy(x_second[b], x_table[1][:].indirect(entries))

        def hidden(b, g):
            moving = x_first[:, rows(b)] if g == 0 else x_second[b]
            for n in range(PACK):
                u, i = divmod(n, PAIR)
                nc.tensor.matmul_mx(
                    out=h_acc[b][:, PAIR_FIRST[g][u] + i, :],
                    lhsT=w_codes[g][u][:, rows(i)].bitcast(FP8X4),
                    lhsT_scale=w_scale[g][u][:, rows(i)],
                    rhs=moving.bitcast(FP8X4),
                    rhs_scale=x_scale[PACK * g : P, rows(b)],
                    start=g == 0 and n == 0,
                    stop=g == PASSES - 1 and n == PACK - 1,
                )

        def rectify(b):
            group, slot = place[b]
            dst = h_grouped[group][:, slot].rearrange("p (c i) t -> p c t i", i=PAIR)
            src = h_acc[b][:].rearrange("p t (c i) -> p c t i", i=PAIR)
            if b == LAST:
                nc.vector.tensor_scalar_max(dst, src, 0.0)
            else:
                nc.scalar.activation(dst, src, ACT.Relu)

        def quantize_h(group):
            nc.vector.quantize_mx(
                h_codes[group][:].bitcast(FP8X4), h_scale[group][:], h_grouped[group][:].rearrange("p b n t -> p (b n t)")
            )

        def score(b):
            group, slot = place[b]
            nc.tensor.matmul_mx(
                out=y_acc[b][:],
                lhsT=h_codes[group][:, rows(slot)].bitcast(FP8X4),
                lhsT_scale=h_scale[group][:, rows(slot)],
                rhs=e_codes[:].bitcast(FP8X4),
                rhs_scale=e_scale[:],
                start=True,
                stop=True,
            )

        def share(turn, b):
            if turn == 1:
                gg = placed([P, V], F32, f"gg{b}", decay_at + ROW // 2)
            else:
                gg = tile([P, V], F32, f"gg{b}", tag=f"total{SUM_ORDER[turn - 2]}" if turn else None)
            total = tile([P, 1], F32, f"total{b}")
            if b == LAST:
                nc.vector.scalar_tensor_tensor(gg[:], y_acc[b][:], 0.0, partial[b][:], ALU.max, ALU.mult, accum_out=total[:])
            else:
                nc.vector.scalar_tensor_tensor(gg[:], partial[b][:], 1.0, before_sb[b][:], ALU.mult, ALU.mult, accum_out=total[:])
            lam_part = tile([P, 1], F32, f"lam_part{b}")
            nc.scalar.activation(lam_part[:], total[:], ACT.Identity, bias=mu_part[:, b : b + 1], scale=1.0 / GAIN)
            factor = tile([P, 1], F32, f"factor{b}")
            nc.vector.reciprocal(factor[:], lam_part[:])
            return gg, factor

        def finish(b, gg, factor):
            parts = LAST_PARTS if b == SUM_ORDER[-1] else 1
            width = V // parts
            for c in range(parts):
                cols = slice(c * width, (c + 1) * width)
                result = tile([P, width], F32, f"result{b}_{c}")
                nc.scalar.activation(result[:], gg[:, cols], ACT.Ln, bias=floor[:], scale=factor[:])
                nc.sync.dma_start(out[rows(b), cols], result[:])

        nc.gpsimd.memset(x_scale_table[:].bitcast(I32), 0)
        nc.vector.memset(e_scale_table[:].bitcast(I32), 0)
        nc.gpsimd.memset(ones[:], 1.0)
        nc.scalar.activation(exp_floor[:], ones[:], ACT.Copy, scale=math.exp(FLOOR))
        nc.gpsimd.memset(mu_rows[:], 0.0)
        nc.gpsimd.dma_start(e_scale_table[0:P:E_STEP, :].bitcast(I32), e_scales[0].bitcast(I32))
        nc.gpsimd.memset(e_scale[:].bitcast(I32), 0)

        load_x(0)
        nc.sync.dma_start(x_list[:], offs)
        load_x_scales()
        load_w(0)
        nc.sync.dma_start(e_list[:], past)
        nc.sync.dma_start(mu_rows[:BLOCKS, :], mu.rearrange("(b p) o -> b (p o)", p=P))
        load_w(1)
        load_x(1)
        nc.sync.dma_start(e_table[:].bitcast(I32), e_words[0].rearrange("p n t -> p (n t)").bitcast(I32))
        make_identity(nc, identity[:])
        mu_turned = psum.tile([P, P], F32, name="mu_turned", tag=f"y_acc{LAST}")
        nc.tensor.transpose(mu_turned[:], mu_rows[:], identity[:])
        nc.scalar.activation(mu_part[:], mu_turned[:, :BLOCKS], ACT.Copy, scale=1.0 / GAIN)
        y_acc = [psum.tile([P, V], F32, name=f"y_acc{b}", tag=f"y_acc{b}") for b in range(BLOCKS)]

        nc.vector.tensor_copy(x_scale[:], x_scale_table[:].indirect(x_list[:]))
        nc.vector.tensor_copy(x_first[:], x_table[0][:].indirect(x_list[:]))
        round_w(0)
        nc.vector.tensor_copy(e_picked[:], e_scale_table[:].indirect(e_list[:]))
        move_e_scales()
        quantize_w(0)
        for b in range(BLOCKS):
            hidden(b, 0)
        round_w(1)
        quantize_w(1)
        nc.sync.dma_start(ago_upper[:], ago.rearrange("(b p) v -> p b v", p=P)[:, PAIR:, :])
        for b in DECAY_ORDER[PAIR:]:
            nc.sync.dma_start(ago_sb[b], ago[rows(b), :])
        for b in SUM_ORDER[:-1]:
            nc.sync.dma_start(before_sb[b][:], before[rows(b), :])
        for b in range(BLOCKS):
            gather_x_second(b)
            hidden(b, 1)
            if b != LAST:
                rectify(b)
        nc.sync.dma_start(before_sb[SUM_ORDER[-1]][:], before[rows(SUM_ORDER[-1]), :])
        nc.vector.tensor_copy(e_codes[:], e_table[:].indirect(e_list[:]))
        for group, bs in enumerate(H_GROUPS):
            if group == 1:
                rectify(LAST)
            quantize_h(group)
            for b in bs:
                score(b)
        for b in DECAY_ORDER:
            nc.scalar.activation(decay[b][:], ago_sb[b], ACT.Exp, scale=-RATE)
        nc.gpsimd.tensor_tensor(partial[LAST][:], decay[LAST][:], before_sb[LAST][:], ALU.mult)
        for b in SUM_ORDER[1:]:
            nc.vector.scalar_tensor_tensor(partial[b][:], y_acc[b][:], 0.0, decay[b][:], ALU.max, ALU.mult)
        nc.scalar.activation(floor[:], exp_floor[:], ACT.Ln)
        shares = [share(turn, b) for turn, b in enumerate(SUM_ORDER)]
        for b, (gg, factor) in zip(SUM_ORDER, shares):
            finish(b, gg, factor)
